import numpy as np, ml_dtypes
CORES = [16,18,20,22]
N = 4
import mx_ref
BF = ml_dtypes.bfloat16
def gentries(a):
    return np.ascontiguousarray(a.reshape(8, 16, -1).transpose(0, 2, 1)).reshape(8, -1)
def gtable(e):
    e = np.asarray(e); return np.ascontiguousarray(e.reshape(8, -1, 16).transpose(0, 2, 1)).reshape(128, -1).astype(np.int32)
def gcols(t, e):
    v = np.concatenate([t.reshape(8, 16, -1, 4), np.zeros((8, 16, 1, 4), BF)], axis=2)
    return np.ascontiguousarray(np.stack([v[g][:, e[g]] for g in range(8)])).reshape(128, -1)
def gpick(z, e):
    return np.concatenate([z[16 * g:16 * g + 16][:, e[g]] for g in range(8)])
def tile(rs):
    return np.stack(rs, axis=2).reshape(128, -1).astype(BF)
def pick(q, e):
    c = np.concatenate([q[0].reshape(128, -1, 4), np.zeros((128, 1, 4), np.uint8)], axis=1); s = np.concatenate([q[1], np.ones((16, 1), np.uint8)], axis=1)
    return (np.ascontiguousarray(c[:, e].reshape(128, -1)), np.ascontiguousarray(s[:, e]))
def join(*qs):
    return (np.concatenate([q[0] for q in qs], axis=1), np.concatenate([q[1] for q in qs], axis=1))
def put(q, e, v):
    c, s = q[0].reshape(128, -1, 4).copy(), q[1].copy(); c[:, e] = v[0].reshape(128, -1, 4); s[:, e] = v[1]
    return (c.reshape(128, -1), s)
def pk(c, s):
    return (np.ascontiguousarray(c), mx_ref.live(s))
def emit(q):
    return q[0], q[1]
def packed(v, rng):
    q = [mx_ref.quantize(np.ascontiguousarray(v[r])) for r in range(N)]
    return np.stack([a for a, b in q]), np.stack([mx_ref.plane(b, rng) for a, b in q])
def values_of_codes():
    e, c = np.zeros((128, 128, 4), np.float32), np.zeros((128, 2, 4), np.uint8)
    e[np.arange(128), np.arange(128), 0] = 1
    c[:127, :, 0] = np.arange(256).reshape(2, 128).T[:127]
    return mx_ref.matmul(mx_ref.quantize(e.reshape(128, 512).astype(BF)), (c.reshape(128, 8), np.full((16, 2), 127, np.uint8))).T.reshape(-1).astype(np.float64)
CODE_VALUE, SCALE_VALUE = values_of_codes(), 2.0 ** (np.arange(256) - 127.0)
def decode(q):
    return (CODE_VALUE[q[0]].reshape(16, 8, -1, 4) * SCALE_VALUE[q[1]][:, None, :, None] + 0.0).reshape(128, -1).astype(np.float32)
def f(rng, *shape):
    return mx_ref.flush((rng.standard_normal(shape, dtype=np.float32) * np.exp2(rng.integers(-2, 3, shape[:-1] + (1,)))).astype(BF))
def wide(rng, *shape, cols=0):
    v = rng.standard_normal(shape, dtype=np.float32) * np.exp2(rng.integers(-12, 13, shape)).astype(np.float32)
    if cols: v *= np.repeat(np.exp2(rng.integers(-cols, cols + 1, shape[:-2] + (1, shape[-1] // 4))) * (rng.random(shape[:-2] + (1, shape[-1] // 4)) > 0.0625), 4, axis=-1).astype(np.float32)
    return mx_ref.flush(v.astype(BF))
C = 448
STEP = [1, 2, 3]
def numbers_of(rng):
    return {"x": np.array(f(rng, N, 128, 4 * C)), "u": np.array(f(rng, N, 128, 512)), "v": np.array(f(rng, N, 128, 512))}
def stored(k):
    return {"od": np.stack([gtable(k[r]) for r in range(N)])}
def orders(rng):
    return stored(rng.permuted(np.tile(np.arange(C), (N, 8, 1)), axis=2))
def rings(rng):
    h = rng.permutation(8)
    pairs = [1] + [2] * (C // 2 - 1) + [1]
    sizes = [[C], [C], [1, C - 1], [257, C - 257], pairs, pairs, [C // 2, C // 2], [1] * C]
    i = np.arange(N)
    odd = (i ^ (i >> 1) ^ (i >> 2)) % 2
    k = np.zeros((N, 8, C), np.int64)
    for g in range(8):
        w = np.arange(C) if h[g] % 2 == 0 else rng.permutation(C)
        c, after = rng.permutation(C), np.zeros(C, np.int64)
        a = 0
        for m in sizes[h[g]]:
            after[w[a:a + m]] = np.roll(w[a:a + m], -1)
            a += m
        k[:, g] = np.where(odd[:, None] == 1, c[after], c)
    return stored(k)
def layers(rng):
    return np.array(f(rng, N, 128, 2048)).reshape(N, 8, 16, 4, 8, 16, 4)
def weights(rng, w):
    c, s = packed(np.ascontiguousarray(w).reshape(N, 128, 2048), rng)
    return {"wc": c, "ws": s}
def setup_inputs(rng):
    return {**numbers_of(rng), **orders(rng), **weights(rng, layers(rng))}
def setup_inputs_ties(rng):
    d = numbers_of(rng)
    o = rng.permutation(N)
    k = rng.integers(-1, 2, (N, 8, C)).astype(np.float32)
    k[o[0]] = 0
    k[o[1]] = 1
    k[o[2]] = -1
    x = d["x"].reshape(N, 8, 16, C, 4)
    x[:, :, 0] = 0
    x[:, :, 0, :, 0] = k.astype(BF)
    u = d["u"].reshape(N, 128, 128, 4)
    u[:, :, ::16] = 0
    for h in range(0, 128, 16): u[:, h, h, 0] = 1
    w = layers(rng)
    w[:, :, :, :, :, 0] = 0
    return {"x": x.reshape(N, 128, 4 * C), "u": u.reshape(N, 128, 512), "v": d["v"], **rings(rng), **weights(rng, w)}
def setup_inputs_near(rng):
    d = numbers_of(rng)
    small = ((np.arange(N) & STEP[1]) > 0) ^ (rng.random() < 0.5)
    k = np.where(small, 2.0 ** -30, 1.0)
    x = d["x"].astype(np.float32).reshape(N, 8, 16, C, 4)
    x[:, :, :8] = 0
    s = rng.integers(-1, 2, (N, 8, C)) * k[:, None, None]
    x[:, :, 0, :, 0] = 1.125 * s
    x[:, :, 1, :, 0] = -1.25 * s
    x[:, :, 2, :, 0] = rng.choice([-1.0, 1.0], (N, 8, C)) * 2.0 ** -30
    x[:, :, 4, :, 0] = 2.0 ** -30
    for r in range(N):
        at = [0, C - 1, int(rng.integers(C)), int(rng.integers(C))]
        for g, j in zip(rng.permutation(8)[:4], at): x[r, g, 0, j, 0] = 2.0 ** 30 * rng.choice([-1.0, 1.0])
    k = k.astype(np.float32)
    u = d["u"].reshape(N, 128, 128, 4)
    u[:, :, ::16] = 0
    for h in range(0, 128, 16):
        u[:, h, h, 0] = (1.125 * k).astype(BF)
        u[:, h + 1, h, 0] = k.astype(BF)
        u[:, h + 3, h, 0] = k.astype(BF)
    w = layers(rng)
    w[:, :, :8] = 0
    w[:, :, :, :, :, :8] = 0
    for r in range(N):
        for g in range(8):
            if small[r]: w[r, g, 2, 0, g, 3, 0] = 2.0 ** -8
    return {"x": x.reshape(N, 128, 4 * C).astype(BF), "u": u.reshape(N, 128, 512), "v": d["v"], **orders(rng), **weights(rng, w)}
def setup_inputs_odd(rng):
    d = numbers_of(rng)
    x = (1.0 + (2 * rng.integers(0, 64, (N, 16, 8, C, 4)) + 1) * 2.0 ** -7) * np.exp2(-rng.integers(0, 7, (N, 16, 8, C, 4)).astype(np.float64)) * rng.choice([-1.0, 1.0], (N, 16, 8, C, 4))
    x[:, :, 0, :, 0] = np.where(rng.random((N, 16, C)) < 0.5, 1.96875, 1.875) * 2.0 ** 8 * rng.choice([-1.0, 1.0], (N, 16, 1))
    x[:, ::2, 1, :, 0] = rng.integers(7, 10, (N, 8, C)) * 2.0 ** -8
    x[:, ::2, 2, :, 0] = -8 * 2.0 ** -8
    u = d["u"].reshape(N, 16, 8, 128, 4)
    u[:, :, :, ::16] = 0
    for g in range(8): u[:, 2 * g, 1:3, 16 * g, 0] = 1
    w = layers(rng)
    for i in (0, 8):
        w[:, :, i] = 0
        w[:, :, :, :, :, i] = 0
    return {"x": x.astype(np.float32).reshape(N, 128, 4 * C).astype(BF), "u": u.reshape(N, 128, 512), "v": d["v"], **orders(rng), **weights(rng, w)}
def setup_inputs_ends(rng):
    d = numbers_of(rng)
    o, most = rng.permutation(N) % 4, rng.permutation(N) % 2
    h, e = rng.permutation(8), int(rng.integers(8))
    c = np.where(h < 2, 0.0, h % 2 * 2.0 - 1.0)[None, :, None]
    k = np.array([2.0, 4.0])[rng.permutation(8) % 2]
    x = np.zeros((N, 8, 16, C, 4))
    u = d["u"].astype(np.float32).reshape(N, 128, 128, 4)
    v = np.zeros((N, 128, 512), np.float32)
    w = np.zeros((N, 128, 4, 128, 4), np.float32)
    i = np.arange(128)
    for r in range(N):
        low = -0.7 * (0.9 + 0.1 * rng.random((8, 16, C, 4))) * 2.0 ** 30
        tiny = -(1.0 + 0.125 * rng.integers(0, 8, (8, 16, C, 4))) * 2.0 ** -30
        if o[r] == 0: x[r] = low
        if o[r] == 1: x[r] = np.where((rng.random(C) < 0.5)[:, None], 0.7 * (1.0 + 0.4 * rng.random((8, 16, C, 4))) * 2.0 ** 27, low)
        if o[r] == 2: x[r] = tiny
        if o[r] == 3: x[r] = d["x"][r].astype(np.float32).reshape(8, 16, C, 4)[:, :, :1]
        x[r, e, 8:] = tiny[e, 8:, :1] if o[r] == 3 else tiny[e, 8:]
        if o[r] < 2: u[r, :, ::16] = c * (0.9 + 0.1 * rng.random((128, 8, 4))) * 2.0 ** 30
        if o[r] == 2: u[r, :, ::16] = c * (1.0 + 0.125 * rng.integers(0, 8, (128, 8, 4))) * 2.0 ** -30
        if o[r] == 3: u[r, :, ::16] *= np.abs(c).astype(np.float32)
        a = (0.9 + 0.1 * rng.random((128, 512))) * 2.0 ** 30 if o[r] < 2 else (1.0 + 0.125 * rng.integers(0, 8, (128, 512))) * 2.0 ** -30
        v[r] = rng.choice([-1.0, 1.0], (128, 512)) * a
        t = k[i // 16]
        t[16 * e + 8:16 * e + 16] = 2.0 ** 8 if most[r] else 2.0 ** -8
        for b in range(4): w[r, i, b, i, b] = t
    return {"x": x.astype(np.float32).reshape(N, 128, 4 * C).astype(BF), "u": u.reshape(N, 128, 512).astype(BF), "v": v.astype(BF), **rings(rng), **weights(rng, w.astype(BF))}
def setup_inputs_spread(rng):
    d = setup_inputs(rng)
    d["x"] = wide(rng, N, 128, 4 * C, cols=6)
    return d
def check_inputs(d):
    b = []
    for k in ("x", "u", "v"):
        a = np.abs(d[k].astype(np.float32))
        if not (np.isfinite(a).all() and ((a == 0) | (a >= 2.0 ** -30) & (a <= 2.0 ** 30)).all()): b.append("a value of " + k)
    none, least, most = [emit(mx_ref.quantize(np.full((128, 16), k, np.float32).astype(BF)))[1][0, 0] for k in (0.0, 2.0 ** -8, 2.0 ** 8)]
    for r in range(N):
        if not (np.sort(gentries(d["od"][r]), axis=1) == np.arange(C)).all(): b.append("od: a group whose entries are not all columns once")
        if ((d["wc"][r] == 0x7F) | (d["wc"][r] == 0xFF)).any(): b.append("wc: a code that is no number")
        s = mx_ref.live(d["ws"][r])
        if ((s != none) & ((s < least) | (s > most))).any(): b.append("ws: a scale out of range")
        if (((d["wc"][r].reshape(16, 8, 512, 4) & 0x7F) != 0) & (s == none)[:, None, :, None]).any(): b.append("wc: a code other than zero under the scale of zeros")
    return b
def at(t, e):
    return np.take_along_axis(t, e, axis=1)
def reference(x, u, v, od, wc, ws):
    qu = [mx_ref.quantize(u[r]) for r in range(N)]
    lay = [pk(wc[r], ws[r]) for r in range(N)]
    now = [x[r] for r in range(N)]
    order = [gentries(od[r]).astype(np.int64) for r in range(N)]
    for step in STEP:
        old, order, far, z = order, [], [], []
        for r in range(N):
            q = mx_ref.quantize(now[r])
            s = mx_ref.matmul(qu[r], q)[::16]
            mine, other = old[r], old[r ^ step]
            jump = at(np.argsort(other, axis=1), mine)
            low = np.tile(np.arange(C), (8, 1))
            for i in range(9):
                low = np.minimum(low, at(low, jump))
                jump = at(jump, jump)
            order.append(np.where(at(s, at(mine, low)) > 0, other, mine))
            far.append(decode(q))
            t = far[r].astype(BF)
            pair = gcols(t, order[r]).astype(np.float32) + gcols(t, at(order[r], order[r])).astype(np.float32)
            z.append(mx_ref.quantize((pair * np.float32(0.5)).astype(BF)))
        for r in range(N):
            back = np.argsort(order[r], axis=1)
            now[r] = tile([gpick(mx_ref.matmul(pick(lay[r], np.arange(128 * b, 128 * b + 128)), z[r ^ step]) * np.float32(0.03125), back) + far[r][:, b::4] for b in range(4)])
    y, fo = np.zeros((N, 128, C), np.float32), np.zeros((N, 8, C), np.float32)
    oc, osc = np.zeros((N, 128, 4 * C), np.uint8), np.zeros((N, 16, C), np.uint8)
    for r in range(N):
        q = mx_ref.quantize(now[r])
        y[r] = mx_ref.matmul(mx_ref.quantize(v[r]), q)
        fo[r] = order[r]
        oc[r], osc[r] = emit(q)
    return {"y": y, "fo": fo, "oc": oc, "osc": osc}

@@ -1,0 +1,350 @@
+from concourse.mybir import dt, AluOpType, ActivationFunctionType
+
+C = 448
+K = C // 16
+STEP = [1, 2, 3]
+RADIX = [3, 3, 3, 3, 3, 2]
+MID = C // 2
+UP = 512.0
+SCN = "float16"
+
+SCRATCH = {
+    "md": ("sbuf", [128, C], "int32"), "rti": ("sbuf", [128, C], "int32"),
+    "thr": ("sbuf", [128, C], "float32"), "d0": ("sbuf", [128, C], "bfloat16"),
+    "da": ("sbuf", [128, C], "bfloat16"), "db": ("sbuf", [128, C], "bfloat16"),
+    "rst": ("sbuf", [128, C], "bfloat16"), "iots": ("sbuf", [128, C], "bfloat16"),
+    "iotd": ("sbuf", [128, C], "bfloat16"), "iotf": ("sbuf", [128, C], "float32"), "ones": ("sbuf", [128, 516], "bfloat16"),
+    "eye": ("sbuf", [128, 516], "bfloat16"), "bia": ("sbuf", [128, 4], "float32"),
+    "uoi": ("sbuf", [128, 8], "int32"), "uo": ("sbuf", [128, 8], "uint16"),
+    "odl": ("sbuf", [128, K], "int32"), "ut": ("sbuf", [128, 512], "bfloat16"),
+    "vt": ("sbuf", [128, 512], "bfloat16"), "xt0": ("sbuf", [128, 4 * C], "bfloat16"),
+    "qu": ("sbuf", [128, 128], "float8_e4m3fn_x4"), "su": ("sbuf", [128, 128], "uint8"),
+    "qur": ("sbuf", [128, 128], "float8_e4m3fn_x4"), "sur": ("sbuf", [128, 128], "uint8"),
+    "qv": ("sbuf", [128, 128], "float8_e4m3fn_x4"), "sv": ("sbuf", [128, 128], "uint8"),
+    "qe": ("sbuf", [128, 512], "float8_e4m3fn_x4"), "se": ("sbuf", [128, 512], "uint8"),
+    "wq": ("sbuf", [128, 512], "float8_e4m3fn_x4"), "wp": ("sbuf", [128, 512], "uint8"),
+    "odr": ("sbuf", [128, K], "int32"),
+    "sc": ("sbuf", [128, C], "float32"), "so": ("sbuf", [128, C], "float32"),
+    "dm": ("sbuf", [128, C], "bfloat16"), "ds": ("sbuf", [128, C], "bfloat16"),
+    "bs1": ("sbuf", [128, C], "bfloat16"),
+    "zt": ("sbuf", [128, 4 * C], "bfloat16"), "xt": ("sbuf", [128, 4 * C], "bfloat16"),
+    "ysb": ("sbuf", [128, C], "float32"), "osp": ("sbuf", [128, C], "float32"),
+    "tu": ("sbuf", [128, K * 40], "uint16"), "tf": ("sbuf", [128, K * 20], "float32"),
+    "pa": ("psum", [128, 2048], "float32"), "pb": ("psum", [128, 2048], "float32"),
+}
+for _b in range(4):
+    SCRATCH["f%d" % _b] = ("sbuf", [128, C], "bfloat16")
+    SCRATCH["fd%d" % _b] = ("sbuf", [128, C], "bfloat16")
+    SCRATCH["u%d" % _b] = ("sbuf", [128, C], "float32")
+    SCRATCH["ld%d" % _b] = ("sbuf", [128, C], "bfloat16")
+    SCRATCH["r%d" % _b] = ("sbuf", [128, C], "float32")
+    SCRATCH["scn%d" % _b] = ("sbuf", [128, C], SCN)
+    SCRATCH["kb%d" % _b] = ("sbuf", [128, C], "bfloat16")
+    SCRATCH["lb%d" % _b] = ("sbuf", [128, C], "bfloat16")
+    SCRATCH["xq%d" % _b] = ("sbuf", [128, C], "float8_e4m3fn_x4")
+    SCRATCH["xs%d" % _b] = ("sbuf", [128, C], "uint8")
+for _n in (1, 2, 3):
+    SCRATCH["zq%d" % _n] = ("sbuf", [128, C], "float8_e4m3fn_x4")
+    SCRATCH["zs%d" % _n] = ("sbuf", [128, C], "uint8")
+    SCRATCH["zl%d" % _n] = ("sbuf", [128, C], "float8_e4m3fn_x4")
+    SCRATCH["zp%d" % _n] = ("sbuf", [128, C], "uint8")
+    SCRATCH["bk%d" % _n] = ("sbuf", [128, C], "bfloat16")
+for _n in (2, 3):
+    SCRATCH["bs%d" % _n] = ("sbuf", [128, C], "bfloat16")
+    SCRATCH["ol%d" % _n] = ("sbuf", [128, K], "uint16")
+
+SEMAPHORES = ["cv", "cs", "ct", "cg", "sent", "a_od"] \
+    + ["a_z%d" % n for n in (1, 2, 3)] + ["a_bs%d" % n for n in (2, 3)] + ["a_ol%d" % n for n in (2, 3)] \
+    + ["l_" + n for n in ("od", "x", "u", "v", "wc", "ws", "y0", "y1", "fo", "oc", "osc", "f0", "f1", "f2", "f3")]
+
+ADD, MUL, SUB, MIN, MAX = AluOpType.add, AluOpType.mult, AluOpType.subtract, AluOpType.min, AluOpType.max
+COPY = ActivationFunctionType.Copy
+
+
+def rank_program(g, core, T, topo):
+    rank = T.rank_of(core)
+    if rank is None:
+        return
+    queues = {"v": g.vector, "s": g.scalar, "t": g.tensor, "g": g, "y": g.sync}
+    count = {"v": 0, "s": 0, "t": 0, "g": 0}
+    wrote, read, snap = {}, {}, {}
+    seen = {q: {} for q in queues}
+    totals = {}
+
+    def learn(q, sem, val):
+        s = seen[q]
+        if s.get(sem, 0) < val:
+            s[sem] = val
+        for a, b in snap.get((sem, val), {}).items():
+            if s.get(a, 0) < b:
+                s[a] = b
+
+    def await_for(q, reads, writes):
+        need = {}
+        for k in reads:
+            for sem, val in wrote.get(k, []):
+                need[sem] = max(need.get(sem, 0), val)
+        for k in writes:
+            for sem, val in wrote.get(k, []):
+                need[sem] = max(need.get(sem, 0), val)
+            for sem, val in read.get(k, []):
+                need[sem] = max(need.get(sem, 0), val)
+        for sem in sorted(need):
+            if seen[q].get(sem, 0) < need[sem]:
+                queues[q].wait_ge(T.sem[sem], need[sem])
+                learn(q, sem, need[sem])
+
+    def note(q, tok, reads, writes):
+        snap[tok] = dict(seen[q])
+        for k in reads:
+            read.setdefault(k, []).append(tok)
+        for k in writes:
+            wrote[k] = [tok]
+            read[k] = []
+
+    def op(q, reads, writes, call):
+        await_for(q, reads, writes)
+        count[q] += 1
+        sem = "c" + q
+        call().then_inc(T.sem[sem], 1)
+        totals[sem] = count[q]
+        note(q, (sem, count[q]), reads, writes)
+
+    def load(q, sem, reads, writes, pairs):
+        await_for(q, reads, writes)
+        for out, in_ in pairs:
+            queues[q].dma_start(out, in_).then_inc(T.sem[sem], 16)
+            totals[sem] = totals.get(sem, 0) + 16
+        note(q, (sem, totals[sem]), reads, writes)
+
+    def peer(step):
+        return T.cores[rank ^ step]
+
+    def bits(engines):
+        return sum(1 << e for e in engines)
+
+    def send(step, out, in_, key, sem, few=False):
+        dst = peer(step)
+        e = topo.engines(core, dst)
+        if few:
+            e = e[::2]
+        await_for("g", [key], [])
+        rid, pid, _ = topo.addr(dst)
+        g.remote_dma(out, in_, T.sem[sem], T.sem["sent"], pid, rid, bits(e))
+        totals["sent"] = totals.get("sent", 0) + len(e)
+        return len(e)
+
+    def arrives(sem, engines, keys):
+        totals[sem] = totals.get(sem, 0) + engines
+        for k in keys:
+            wrote[k] = [(sem, totals[sem])]
+        if len(keys) > 0:
+            snap.setdefault((sem, totals[sem]), {})
+
+    V, S = g.vector, g.scalar
+    slots, fslots = [0], [0]
+
+    def slot():
+        slots[0] += 1
+        return slots[0] - 1
+
+    def fslot():
+        fslots[0] += 1
+        return fslots[0] - 1
+
+    def tu(i):
+        return T.tu[:, K * i:K * (i + 1)]
+
+    def tf(i):
+        return T.tf[:, K * i:K * (i + 1)]
+
+    def by(name, i):
+        return T[name][:, 0:C].indirect(tu(i))
+
+    def tok(i):
+        return "tu%d" % i
+
+    load("y", "l_od", [], ["odl"], [(T.odl[:], T.od[:])])
+    load("y", "l_u", [], ["ut"], [(T.ut[:], T.u[:])])
+    load("y", "l_x", [], ["xt0"], [(T.xt0[:], T.x[:])])
+    load("y", "l_wc", [], ["wq"], [(T.wq[:, 0:512].bitcast(dt.uint8), T.wc[:, 0:2048])])
+    load("y", "l_ws", [], ["wp"], [(T.wp[:, 0:512], T.ws[:, 0:512])])
+    load("y", "l_v", [], ["vt"], [(T.vt[:], T.v[:])])
+
+    op("g", [], ["md"], lambda: g.iota(T.md[:], [[1, C]], 128, -1))
+    op("g", [], ["iots"], lambda: g.iota(T.iots[:], [[1, C]], -MID, 0, allow_small_or_imprecise_dtypes=True))
+    op("v", [], ["ones"], lambda: V.memset(T.ones[:], 1.0))
+    arrives("a_od", send(STEP[0], T.odr[:], T.odl[:], "odl", "a_od", few=True), ["odr"])
+    op("g", ["ones"], ["eye"], lambda: g.affine_select(T.eye[:], T.ones[:], [[1, 516]], AluOpType.is_equal, 0.0, -3, -4))
+    op("g", [], ["uoi"], lambda: g.iota(T.uoi[:], [[16, 8]], 0, 0))
+    op("g", [], ["rti"], lambda: g.iota(T.rti[:], [[0, K], [1, 16]], 0, 0))
+    op("g", [], ["iotf"], lambda: g.iota(T.iotf[:], [[1, C]], 0, 0, allow_small_or_imprecise_dtypes=True))
+
+    op("v", ["md"], ["md"], lambda: V.tensor_scalar(T.md[:], T.md[:], 15, None, AluOpType.bitwise_and))
+    op("v", ["md"], ["da"], lambda: V.tensor_scalar(T.da[:], T.md[:], 1.0, UP, AluOpType.is_equal, MUL))
+    op("v", ["md"], ["db"], lambda: V.tensor_scalar(T.db[:], T.md[:], 0.0, -2 * UP, AluOpType.is_equal, MUL))
+    op("v", ["da", "db"], ["d0"], lambda: V.tensor_tensor(T.d0[:], T.da[:], T.db[:], ADD))
+    op("v", ["md"], ["bia0"], lambda: V.tensor_scalar(T.bia[:, 0:1], T.md[:, 15:16], 0.0, UP, AluOpType.is_equal, MUL))
+    op("v", ["bia0"], ["bia"], lambda: V.tensor_scalar(T.bia[:, 1:2], T.bia[:, 0:1], MID - UP, None, ADD))
+    op("v", ["iots"], ["iotd"], lambda: V.tensor_copy(T.iotd[:], T.iots[:]))
+    o_u, o_f = slot(), fslot()
+    op("v", ["odl"], [tok(o_u)], lambda: V.tensor_copy(tu(o_u), T.odl[:]))
+    op("v", ["odl"], ["tf%d" % o_f], lambda: V.tensor_copy(tf(o_f), T.odl[:]))
+    op("v", ["md"], ["thr"], lambda: V.tensor_scalar(T.thr[:], T.md[:], 1.0, 1e29, MIN, MUL))
+
+    def conv(name):
+        i = slot()
+        h = "scn%d" % (i % 4)
+        op("v", [name, "d0"], [h], lambda: V.tensor_tensor_scan(T[h][:], T.d0[:], T[name][:], 0.0, ADD, MAX))
+        op("v", [h, "bia"], [tok(i)], lambda: V.tensor_scalar(tu(i), T[h][:, 15:C:16], T.bia[:, 1:2], None, ADD))
+        return i
+
+    out = {}
+
+    def chain(n, o_u, o_f):
+        star = fslot()
+        delta = fslot()
+        bs = "bs%d" % n
+        if n == 1:
+            su = slot()
+            op("v", ["odr"], [tok(su)], lambda: V.tensor_copy(tu(su), T.odr[:]))
+            op("v", ["iots", tok(su)], [bs], lambda: V.tensor_copy(by(bs, su), T.iots[:]))
+        kn, kname = 0, "kb0"
+        op("s", [bs, tok(o_u)], [kname], lambda: S.activation(T[kname][:], by(bs, o_u), COPY))
+        a = conv(kname)
+        src = "odr" if n == 1 else "ol%d" % n
+        op("v", [src], ["tf%d" % star], lambda: V.tensor_copy(tf(star), T[src][:]))
+        op("v", ["tf%d" % star, "tf%d" % o_f], ["tf%d" % delta], lambda: V.tensor_tensor(tf(delta), tf(star), tf(o_f), SUB))
+        yield
+        low, ln, twin = "iots", 0, "iotd"
+        for j, r in enumerate(RADIX):
+            last = j == len(RADIX) - 1
+            acc = twin
+            cur = kname
+            for e in range(r - 1):
+                if not last:
+                    kn = (kn + 1) % 4
+                    new = "kb%d" % kn
+                    op("s", [cur, tok(a)], [new], lambda: S.activation(T[new][:], by(cur, a), COPY))
+                    cur = new
+                ln = (ln + 1) % 4
+                lnew = "lb%d" % ln
+                op("v", [acc, low, tok(a)], [lnew], lambda: V.tensor_tensor(T[lnew][:], by(acc, a), T[low][:], MIN))
+                acc = lnew
+            low = acc
+            kname = cur
+            if not last:
+                twin = "ld%d" % (j % 4)
+                op("s", [low], [twin], lambda: S.activation(T[twin][:], T[low][:], COPY))
+                a = conv(kname)
+            yield
+        out["low"] = conv(low)
+        out["delta"] = delta
+        yield
+
+    def unpack_products(n):
+        xq, xs = "xq%d" % n, "xs%d" % n
+        op("t", ["qur", xq], ["pb0"], lambda: g.tensor.matmul_mx(T.pb[:, 0:C], T.qur[:, 0:128], T.sur[:, 0:128], T[xq][:, 0:C], T[xs][:, 0:C], True, True))
+        for b in range(4):
+            op("t", ["qe%d" % b, xq], ["pa%d" % b], lambda: g.tensor.matmul_mx(T.pa[:, 512 * b:512 * b + C], T.qe[:, 128 * b:128 * b + 128], T.se[:, 128 * b:128 * b + 128], T[xq][:, 0:C], T[xs][:, 0:C], True, True))
+
+    def f_copy(b):
+        op("s", ["pa%d" % b], ["f%d" % b], lambda: S.activation(T["f%d" % b][:], T.pa[:, 512 * b:512 * b + C], COPY))
+        load("y", "l_f%d" % b, ["f%d" % b], ["fd%d" % b], [(T["fd%d" % b][:], T["f%d" % b][:])])
+
+    def scores(o_u):
+        op("s", ["pb0"], ["sc"], lambda: S.activation(T.sc[:], T.pb[:, 0:C], COPY))
+        op("s", ["sc", tok(o_u)], ["so"], lambda: S.activation(T.so[:], by("sc", o_u), COPY))
+
+    def choose(o_f):
+        low, delta = out["low"], out["delta"]
+        t, nf, nu = fslot(), fslot(), slot()
+        op("v", ["so", "thr", tok(low)], ["dm"], lambda: V.tensor_tensor(T.dm[:], by("so", low), T.thr[:], AluOpType.is_gt))
+        op("v", ["dm", "rst"], ["ds"], lambda: V.tensor_tensor_scan(T.ds[:], T.rst[:], T.dm[:], 0.0, MUL, ADD))
+        op("v", ["ds", "tf%d" % delta], ["tf%d" % t], lambda: V.tensor_tensor(tf(t), T.ds[:, 15:C:16], tf(delta), MUL))
+        op("v", ["tf%d" % t, "tf%d" % o_f], ["tf%d" % nf], lambda: V.tensor_tensor(tf(nf), tf(t), tf(o_f), ADD))
+        op("v", ["tf%d" % nf], [tok(nu)], lambda: V.tensor_copy(tu(nu), tf(nf)))
+        return nu, nf
+
+    def means(n, o_u):
+        for b in range(4):
+            op("v", ["f%d" % b, "fd%d" % b, tok(o_u)], ["u%d" % b], lambda: V.tensor_tensor(T["u%d" % b][:], by("f%d" % b, o_u), T["fd%d" % b][:], ADD))
+            op("s", ["u%d" % b, tok(o_u)], ["zt%d" % b], lambda: S.activation(T.zt[:, b:4 * C:4], by("u%d" % b, o_u), COPY, scale=0.5))
+        bk = "bk%d" % n
+        op("v", ["iots", tok(o_u)], [bk], lambda: V.tensor_copy(by(bk, o_u), T.iots[:]))
+        if n < len(STEP):
+            m = n + 1
+            arrives("a_ol%d" % m, send(STEP[n], T["ol%d" % m][:], tu(o_u), tok(o_u), "a_ol%d" % m, few=True), ["ol%d" % m])
+            arrives("a_bs%d" % m, send(STEP[n], T["bs%d" % m][:], T[bk][:], bk, "a_bs%d" % m, few=True), ["bs%d" % m])
+        zq, zs, zl, zp = "zq%d" % n, "zs%d" % n, "zl%d" % n, "zp%d" % n
+        op("v", ["zt0", "zt1", "zt2", "zt3"], [zq], lambda: V.quantize_mx(T[zq][:, 0:C], T[zs][:, 0:C], T.zt[:, 0:4 * C]))
+        e = send(STEP[n - 1], T[zl][:, 0:C].bitcast(dt.uint8), T[zq][:, 0:C].bitcast(dt.uint8), zq, "a_z%d" % n)
+        e += send(STEP[n - 1], T[zp][:, 0:C], T[zs][:, 0:C], zq, "a_z%d" % n)
+        arrives("a_z%d" % n, e, [zl])
+        return conv(bk)
+
+    def new_state(n, back):
+        zl, zp, xq, xs = "zl%d" % n, "zp%d" % n, "xq%d" % n, "xs%d" % n
+        for b in range(4):
+            op("t", ["wq", "wp", zl], ["pb%d" % b], lambda: g.tensor.matmul_mx(T.pb[:, 512 * b:512 * b + C], T.wq[:, 128 * b:128 * b + 128], T.wp[:, 128 * b:128 * b + 128], T[zl][:, 0:C], T[zp][:, 0:C], True, True))
+            op("s", ["pb%d" % b], ["r%d" % b], lambda: S.activation(T["r%d" % b][:], T.pb[:, 512 * b:512 * b + C], COPY, scale=0.03125))
+            op("v", ["r%d" % b, "f%d" % b, tok(back)], ["xt_%d" % b], lambda: V.tensor_tensor(T.xt[:, b:4 * C:4], by("r%d" % b, back), T["f%d" % b][:], ADD))
+        op("v", ["xt_0", "xt_1", "xt_2", "xt_3"], [xq], lambda: V.quantize_mx(T[xq][:, 0:C], T[xs][:, 0:C], T.xt[:, 0:4 * C]))
+
+    op("v", ["uoi"], ["uo"], lambda: V.tensor_copy(T.uo[:], T.uoi[:]))
+    op("v", ["ut"], ["qu"], lambda: V.quantize_mx(T.qu[:, 0:128], T.su[:, 0:128], T.ut[:, 0:512]))
+    op("v", ["qu", "uo"], ["qur_c"], lambda: V.tensor_copy(T.qur[:, 0:128].bitcast(dt.uint32), T.qu[:, 0:128].bitcast(dt.uint32).indirect(T.uo[:, 0:8])))
+    op("v", ["qu", "uo", "qur_c"], ["qur"], lambda: V.tensor_copy(T.sur[:, 0:128], T.su[:, 0:128].indirect(T.uo[:, 0:8])))
+    for b in range(4):
+        op("v", ["eye"], ["qe%d" % b], lambda: V.quantize_mx(T.qe[:, 128 * b:128 * b + 128], T.se[:, 128 * b:128 * b + 128], T.eye[:, 3 - b:515 - b]))
+    ch = chain(1, o_u, o_f)
+    next(ch)
+    op("v", ["xt0"], ["xq0"], lambda: V.quantize_mx(T.xq0[:, 0:C], T.xs0[:, 0:C], T.xt0[:, 0:4 * C]))
+    unpack_products(0)
+    for b in range(4):
+        next(ch)
+        f_copy(b)
+    op("v", ["rti"], ["rst"], lambda: V.tensor_scalar(T.rst[:], T.rti[:], 1.0, None, MIN))
+    next(ch)
+    scores(o_u)
+    next(ch)
+    next(ch)
+
+    for n in (1, 2, 3):
+        o_u, o_f = choose(o_f)
+        back = means(n, o_u)
+        if n < 3:
+            ch = chain(n + 1, o_u, o_f)
+            for _ in range(3):
+                next(ch)
+            new_state(n, back)
+            unpack_products(n)
+            next(ch)
+            f_copy(0)
+            next(ch)
+            f_copy(1)
+            next(ch)
+            scores(o_u)
+            f_copy(2)
+            next(ch)
+            f_copy(3)
+            next(ch)
+        else:
+            op("v", ["iotf", tok(back)], ["osp"], lambda: V.tensor_copy(by("osp", back), T.iotf[:]))
+            load("y", "l_fo", ["osp"], ["fo"], [(T.fo[:, 0:C], T.osp[0:128:16, 0:C])])
+            op("v", ["vt"], ["qv"], lambda: V.quantize_mx(T.qv[:, 0:128], T.sv[:, 0:128], T.vt[:, 0:512]))
+            new_state(n, back)
+
+    H = C // 2
+    for h in range(2):
+        op("t", ["qv", "xq3"], ["pa%d" % h], lambda: g.tensor.matmul_mx(T.pa[:, 512 * h:512 * h + H], T.qv[:, 0:128], T.sv[:, 0:128], T.xq3[:, H * h:H * h + H], T.xs3[:, H * h:H * h + H], True, True))
+    load("y", "l_oc", ["xq3"], ["oc"], [(T.oc[:, 0:4 * C], T.xq3[:, 0:C].bitcast(dt.uint8))])
+    op("s", ["pa0"], ["ysb0"], lambda: S.activation(T.ysb[:, 0:H], T.pa[:, 0:H], COPY))
+    op("v", ["pa1"], ["ysb1"], lambda: V.tensor_copy(T.ysb[:, H:C], T.pa[:, 512:512 + H]))
+    load("s", "l_y0", ["ysb0"], ["y0"], [(T.y[:, 0:H], T.ysb[:, 0:H])])
+    load("y", "l_y1", ["ysb1"], ["y1"], [(T.y[:, H:C], T.ysb[:, H:C])])
+    load("s", "l_osc", ["xq3"], ["osc"], [(T.osc[4 * k:4 * k + 4, 0:C], T.xs3[32 * k:32 * k + 4, 0:C]) for k in range(4)])
+
+    for sem in sorted(totals):
+        if seen["g"].get(sem, 0) < totals[sem]:
+            g.wait_ge(T.sem[sem], totals[sem])

@@ -3,7 +3,9 @@ from concourse.mybir import dt, AluOpType, ActivationFunctionType
 C = 448
 K = C // 16
 STEP = [1, 2, 3]
-RADIX = [3, 3, 3, 3, 3, 2]
+RADIX = [3, 3, 3, 2, 3, 3]
+PRE = 3
+TV1, TV2 = (0, 1, 2), (1, 2, 3, 4)
 MID = C // 2
 UP = 512.0
 SCN = "float16"
@@ -26,7 +28,7 @@ SCRATCH = {
     "odr": ("sbuf", [128, K], "int32"),
     "sc": ("sbuf", [128, C], "float32"), "so": ("sbuf", [128, C], "float32"),
     "dm": ("sbuf", [128, C], "bfloat16"), "ds": ("sbuf", [128, C], "bfloat16"),
-    "bs1": ("sbuf", [128, C], "bfloat16"),
+
     "zt": ("sbuf", [128, 4 * C], "bfloat16"), "xt": ("sbuf", [128, 4 * C], "bfloat16"),
     "ysb": ("sbuf", [128, C], "float32"), "osp": ("sbuf", [128, C], "float32"),
     "tu": ("sbuf", [128, K * 40], "uint16"), "tf": ("sbuf", [128, K * 20], "float32"),
@@ -43,6 +45,7 @@ for _b in range(4):
     SCRATCH["lb%d" % _b] = ("sbuf", [128, C], "bfloat16")
     SCRATCH["xq%d" % _b] = ("sbuf", [128, C], "float8_e4m3fn_x4")
     SCRATCH["xs%d" % _b] = ("sbuf", [128, C], "uint8")
+SCRATCH["bk0"] = ("sbuf", [128, C], "bfloat16")
 for _n in (1, 2, 3):
     SCRATCH["zq%d" % _n] = ("sbuf", [128, C], "float8_e4m3fn_x4")
     SCRATCH["zs%d" % _n] = ("sbuf", [128, C], "uint8")
@@ -50,12 +53,11 @@ for _n in (1, 2, 3):
     SCRATCH["zp%d" % _n] = ("sbuf", [128, C], "uint8")
     SCRATCH["bk%d" % _n] = ("sbuf", [128, C], "bfloat16")
 for _n in (2, 3):
-    SCRATCH["bs%d" % _n] = ("sbuf", [128, C], "bfloat16")
     SCRATCH["ol%d" % _n] = ("sbuf", [128, K], "uint16")
 
 SEMAPHORES = ["cv", "cs", "ct", "cg", "sent", "a_od"] \
-    + ["a_z%d" % n for n in (1, 2, 3)] + ["a_bs%d" % n for n in (2, 3)] + ["a_ol%d" % n for n in (2, 3)] \
-    + ["l_" + n for n in ("od", "x", "u", "v", "wc", "ws", "y0", "y1", "fo", "oc", "osc", "f0", "f1", "f2", "f3")]
+    + ["a_z10", "a_z20", "a_z30", "a_z31"] + ["a_ol%d" % n for n in (2, 3)] \
+    + ["l_" + n for n in ("od", "x", "u", "v", "wc", "ws", "y0", "y1", "fo", "oc0", "oc1", "osc0", "osc1", "f0", "f1", "f2", "f3")]
 
 ADD, MUL, SUB, MIN, MAX = AluOpType.add, AluOpType.mult, AluOpType.subtract, AluOpType.min, AluOpType.max
 COPY = ActivationFunctionType.Copy
@@ -183,36 +185,40 @@ def rank_program(g, core, T, topo):
     op("v", ["md"], ["md"], lambda: V.tensor_scalar(T.md[:], T.md[:], 15, None, AluOpType.bitwise_and))
     op("v", ["md"], ["da"], lambda: V.tensor_scalar(T.da[:], T.md[:], 1.0, UP, AluOpType.is_equal, MUL))
     op("v", ["md"], ["db"], lambda: V.tensor_scalar(T.db[:], T.md[:], 0.0, -2 * UP, AluOpType.is_equal, MUL))
-    op("v", ["da", "db"], ["d0"], lambda: V.tensor_tensor(T.d0[:], T.da[:], T.db[:], ADD))
-    op("v", ["md"], ["bia0"], lambda: V.tensor_scalar(T.bia[:, 0:1], T.md[:, 15:16], 0.0, UP, AluOpType.is_equal, MUL))
-    op("v", ["bia0"], ["bia"], lambda: V.tensor_scalar(T.bia[:, 1:2], T.bia[:, 0:1], MID - UP, None, ADD))
-    op("v", ["iots"], ["iotd"], lambda: V.tensor_copy(T.iotd[:], T.iots[:]))
     o_u, o_f = slot(), fslot()
     op("v", ["odl"], [tok(o_u)], lambda: V.tensor_copy(tu(o_u), T.odl[:]))
     op("v", ["odl"], ["tf%d" % o_f], lambda: V.tensor_copy(tf(o_f), T.odl[:]))
-    op("v", ["md"], ["thr"], lambda: V.tensor_scalar(T.thr[:], T.md[:], 1.0, 1e29, MIN, MUL))
+    op("v", ["iots", tok(o_u)], ["bk0"], lambda: V.tensor_copy(by("bk0", o_u), T.iots[:]))
+    op("v", ["da", "db"], ["d0"], lambda: V.tensor_tensor(T.d0[:], T.da[:], T.db[:], ADD))
+    op("v", ["md"], ["bia0"], lambda: V.tensor_scalar(T.bia[:, 0:1], T.md[:, 15:16], 0.0, UP, AluOpType.is_equal, MUL))
+    op("v", ["bia0"], ["bia"], lambda: V.tensor_scalar(T.bia[:, 1:2], T.bia[:, 0:1], MID - UP, None, ADD))
 
-    def conv(name):
+    def conv(name, between=None):
         i = slot()
         h = "scn%d" % (i % 4)
         op("v", [name, "d0"], [h], lambda: V.tensor_tensor_scan(T[h][:], T.d0[:], T[name][:], 0.0, ADD, MAX))
+        if between is not None:
+            between()
         op("v", [h, "bia"], [tok(i)], lambda: V.tensor_scalar(tu(i), T[h][:, 15:C:16], T.bia[:, 1:2], None, ADD))
         return i
 
     out = {}
 
-    def chain(n, o_u, o_f):
+    def chain(n, o_u, o_f, twin_v):
         star = fslot()
         delta = fslot()
-        bs = "bs%d" % n
+        bk = "bk%d" % (n - 1)
+        src = "odr" if n == 1 else "ol%d" % n
+        offs, okey = T[src][:, 0:K], src
         if n == 1:
             su = slot()
             op("v", ["odr"], [tok(su)], lambda: V.tensor_copy(tu(su), T.odr[:]))
-            op("v", ["iots", tok(su)], [bs], lambda: V.tensor_copy(by(bs, su), T.iots[:]))
+            offs, okey = tu(su), tok(su)
         kn, kname = 0, "kb0"
-        op("s", [bs, tok(o_u)], [kname], lambda: S.activation(T[kname][:], by(bs, o_u), COPY))
+        op("s", [bk, okey], [kname], lambda: S.activation(T[kname][:], T[bk][:, 0:C].indirect(offs), COPY))
+        if n == 1:
+            yield
         a = conv(kname)
-        src = "odr" if n == 1 else "ol%d" % n
         op("v", [src], ["tf%d" % star], lambda: V.tensor_copy(tf(star), T[src][:]))
         op("v", ["tf%d" % star, "tf%d" % o_f], ["tf%d" % delta], lambda: V.tensor_tensor(tf(delta), tf(star), tf(o_f), SUB))
         yield
@@ -221,12 +227,13 @@ def rank_program(g, core, T, topo):
             last = j == len(RADIX) - 1
             acc = twin
             cur = kname
-            for e in range(r - 1):
-                if not last:
+            if not last:
+                for e in range(r - 1):
                     kn = (kn + 1) % 4
                     new = "kb%d" % kn
                     op("s", [cur, tok(a)], [new], lambda: S.activation(T[new][:], by(cur, a), COPY))
                     cur = new
+            for e in range(r - 1):
                 ln = (ln + 1) % 4
                 lnew = "lb%d" % ln
                 op("v", [acc, low, tok(a)], [lnew], lambda: V.tensor_tensor(T[lnew][:], by(acc, a), T[low][:], MIN))
@@ -235,12 +242,18 @@ def rank_program(g, core, T, topo):
             kname = cur
             if not last:
                 twin = "ld%d" % (j % 4)
-                op("s", [low], [twin], lambda: S.activation(T[twin][:], T[low][:], COPY))
-                a = conv(kname)
+                if j in twin_v:
+                    a = conv(kname, lambda: op("v", [low], [twin], lambda: V.tensor_copy(T[twin][:], T[low][:])))
+                else:
+                    op("s", [low], [twin], lambda: S.activation(T[twin][:], T[low][:], COPY))
+                    a = conv(kname)
             yield
         out["low"] = conv(low)
         out["delta"] = delta
         yield
+
+    def pieces(n):
+        return [(0, C)] if n < len(STEP) else [(0, C // 2), (C // 2, C)]
 
     def unpack_products(n):
         xq, xs = "xq%d" % n, "xs%d" % n
@@ -267,43 +280,77 @@ def rank_program(g, core, T, topo):
         return nu, nf
 
     def means(n, o_u):
-        for b in range(4):
-            op("v", ["f%d" % b, "fd%d" % b, tok(o_u)], ["u%d" % b], lambda: V.tensor_tensor(T["u%d" % b][:], by("f%d" % b, o_u), T["fd%d" % b][:], ADD))
-            op("s", ["u%d" % b, tok(o_u)], ["zt%d" % b], lambda: S.activation(T.zt[:, b:4 * C:4], by("u%d" % b, o_u), COPY, scale=0.5))
         bk = "bk%d" % n
-        op("v", ["iots", tok(o_u)], [bk], lambda: V.tensor_copy(by(bk, o_u), T.iots[:]))
+
+        def inverse():
+            op("v", ["iots", tok(o_u)], [bk], lambda: V.tensor_copy(by(bk, o_u), T.iots[:]))
+
         if n < len(STEP):
             m = n + 1
             arrives("a_ol%d" % m, send(STEP[n], T["ol%d" % m][:], tu(o_u), tok(o_u), "a_ol%d" % m, few=True), ["ol%d" % m])
-            arrives("a_bs%d" % m, send(STEP[n], T["bs%d" % m][:], T[bk][:], bk, "a_bs%d" % m, few=True), ["bs%d" % m])
+        for b in range(4):
+            op("v", ["f%d" % b, "fd%d" % b, tok(o_u)], ["u%d" % b], lambda: V.tensor_tensor(T["u%d" % b][:], by("f%d" % b, o_u), T["fd%d" % b][:], ADD))
+        parts = pieces(n)
+        turn = [(b, 0) for b in range(4)]
+        if len(parts) == 2:
+            turn = [(0, 0), (1, 0), (0, 1), (2, 0), (1, 1), (3, 0), (2, 1), (3, 1)]
+        for b, h in turn:
+            p, e = parts[h]
+            op("s", ["u%d" % b, tok(o_u)], ["zt%d%d" % (b, h)], lambda: S.activation(T.zt[:, 4 * p + b:4 * e:4], T["u%d" % b][:, 0:C].indirect(T.tu[:, K * o_u + p // 16:K * o_u + e // 16]), COPY, scale=0.5))
+        if n < len(STEP):
+            inverse()
         zq, zs, zl, zp = "zq%d" % n, "zs%d" % n, "zl%d" % n, "zp%d" % n
-        op("v", ["zt0", "zt1", "zt2", "zt3"], [zq], lambda: V.quantize_mx(T[zq][:, 0:C], T[zs][:, 0:C], T.zt[:, 0:4 * C]))
-        e = send(STEP[n - 1], T[zl][:, 0:C].bitcast(dt.uint8), T[zq][:, 0:C].bitcast(dt.uint8), zq, "a_z%d" % n)
-        e += send(STEP[n - 1], T[zp][:, 0:C], T[zs][:, 0:C], zq, "a_z%d" % n)
-        arrives("a_z%d" % n, e, [zl])
+        for h, (p, e) in enumerate(parts):
+            key, sem = "%s%d" % (zq, h), "a_z%d%d" % (n, h)
+            op("v", ["zt%d%d" % (b, h) for b in range(4)], [key], lambda: V.quantize_mx(T[zq][:, p:e], T[zs][:, p:e], T.zt[:, 4 * p:4 * e]))
+            k = send(STEP[n - 1], T[zl][:, p:e].bitcast(dt.uint8), T[zq][:, p:e].bitcast(dt.uint8), key, sem)
+            k += send(STEP[n - 1], T[zp][:, p:e], T[zs][:, p:e], key, sem)
+            arrives(sem, k, ["%s%d" % (zl, h)])
+        if n == len(STEP):
+            inverse()
         return conv(bk)
 
     def new_state(n, back):
         zl, zp, xq, xs = "zl%d" % n, "zp%d" % n, "xq%d" % n, "xs%d" % n
-        for b in range(4):
-            op("t", ["wq", "wp", zl], ["pb%d" % b], lambda: g.tensor.matmul_mx(T.pb[:, 512 * b:512 * b + C], T.wq[:, 128 * b:128 * b + 128], T.wp[:, 128 * b:128 * b + 128], T[zl][:, 0:C], T[zp][:, 0:C], True, True))
-            op("s", ["pb%d" % b], ["r%d" % b], lambda: S.activation(T["r%d" % b][:], T.pb[:, 512 * b:512 * b + C], COPY, scale=0.03125))
-            op("v", ["r%d" % b, "f%d" % b, tok(back)], ["xt_%d" % b], lambda: V.tensor_tensor(T.xt[:, b:4 * C:4], by("r%d" % b, back), T["f%d" % b][:], ADD))
-        op("v", ["xt_0", "xt_1", "xt_2", "xt_3"], [xq], lambda: V.quantize_mx(T[xq][:, 0:C], T[xs][:, 0:C], T.xt[:, 0:4 * C]))
+        parts = pieces(n)
+        for h, (p, e) in enumerate(parts):
+            bank = "pb" if h == 0 else "pa"
+            for b in range(4):
+                op("t", ["wq", "wp", "%s%d" % (zl, h)], ["%s%d" % (bank, b)], lambda: g.tensor.matmul_mx(T[bank][:, 512 * b:512 * b + e - p], T.wq[:, 128 * b:128 * b + 128], T.wp[:, 128 * b:128 * b + 128], T[zl][:, p:e], T[zp][:, p:e], True, True))
+                op("s", ["%s%d" % (bank, b)], ["r%d%d" % (b, h)], lambda: S.activation(T["r%d" % b][:, p:e], T[bank][:, 512 * b:512 * b + e - p], COPY, scale=0.03125))
+        for h, (p, e) in enumerate(parts):
+            for b in range(4):
+                op("v", ["r%d%d" % (b, k) for k in range(2)] + ["f%d" % b, tok(back)], ["xt_%d%d" % (b, h)], lambda: V.tensor_tensor(T.xt[:, 4 * p + b:4 * e:4], T["r%d" % b][:, 0:C].indirect(T.tu[:, K * back + p // 16:K * back + e // 16]), T["f%d" % b][:, p:e], ADD))
+            op("v", ["xt_%d%d" % (b, h) for b in range(4)], [xq if n < len(STEP) else "%s%d" % (xq, h)], lambda: V.quantize_mx(T[xq][:, p:e], T[xs][:, p:e], T.xt[:, 4 * p:4 * e]))
+            if n == len(STEP):
+                results(h, p, e)
 
+    def results(h, p, e):
+        key, bank = "xq3%d" % h, "pb%d" % h
+        op("t", ["qv", key], [bank], lambda: g.tensor.matmul_mx(T.pb[:, 512 * h:512 * h + e - p], T.qv[:, 0:128], T.sv[:, 0:128], T.xq3[:, p:e], T.xs3[:, p:e], True, True))
+        load("y", "l_oc%d" % h, [key], [], [(T.oc[:, 4 * p:4 * e], T.xq3[:, p:e].bitcast(dt.uint8))])
+        op("s", [bank], ["ysb%d" % h], lambda: S.activation(T.ysb[:, p:e], T.pb[:, 512 * h:512 * h + e - p], COPY))
+        load("y", "l_y%d" % h, ["ysb%d" % h], [], [(T.y[:, p:e], T.ysb[:, p:e])])
+        load("s", "l_osc%d" % h, [key], [], [(T.osc[4 * k:4 * k + 4, p:e], T.xs3[32 * k:32 * k + 4, p:e]) for k in range(4)])
+
+    ch = chain(1, o_u, o_f, TV1)
+    next(ch)
+    op("v", ["iots"], ["iotd"], lambda: V.tensor_copy(T.iotd[:], T.iots[:]))
     op("v", ["uoi"], ["uo"], lambda: V.tensor_copy(T.uo[:], T.uoi[:]))
     op("v", ["ut"], ["qu"], lambda: V.quantize_mx(T.qu[:, 0:128], T.su[:, 0:128], T.ut[:, 0:512]))
     op("v", ["qu", "uo"], ["qur_c"], lambda: V.tensor_copy(T.qur[:, 0:128].bitcast(dt.uint32), T.qu[:, 0:128].bitcast(dt.uint32).indirect(T.uo[:, 0:8])))
     op("v", ["qu", "uo", "qur_c"], ["qur"], lambda: V.tensor_copy(T.sur[:, 0:128], T.su[:, 0:128].indirect(T.uo[:, 0:8])))
+    next(ch)
     for b in range(4):
         op("v", ["eye"], ["qe%d" % b], lambda: V.quantize_mx(T.qe[:, 128 * b:128 * b + 128], T.se[:, 128 * b:128 * b + 128], T.eye[:, 3 - b:515 - b]))
-    ch = chain(1, o_u, o_f)
     next(ch)
     op("v", ["xt0"], ["xq0"], lambda: V.quantize_mx(T.xq0[:, 0:C], T.xs0[:, 0:C], T.xt0[:, 0:4 * C]))
     unpack_products(0)
     for b in range(4):
-        next(ch)
+        if b > 0:
+            next(ch)
         f_copy(b)
+    op("v", ["md"], ["thr"], lambda: V.tensor_scalar(T.thr[:], T.md[:], 1.0, 1e29, MIN, MUL))
     op("v", ["rti"], ["rst"], lambda: V.tensor_scalar(T.rst[:], T.rti[:], 1.0, None, MIN))
     next(ch)
     scores(o_u)
@@ -314,15 +361,15 @@ def rank_program(g, core, T, topo):
         o_u, o_f = choose(o_f)
         back = means(n, o_u)
         if n < 3:
-            ch = chain(n + 1, o_u, o_f)
-            for _ in range(3):
+            ch = chain(n + 1, o_u, o_f, TV2)
+            for _ in range(PRE):
                 next(ch)
             new_state(n, back)
             unpack_products(n)
-            next(ch)
-            f_copy(0)
-            next(ch)
-            f_copy(1)
+            for b in range(2):
+                if 3 + b >= PRE:
+                    next(ch)
+                f_copy(b)
             next(ch)
             scores(o_u)
             f_copy(2)
@@ -330,20 +377,10 @@ def rank_program(g, core, T, topo):
             f_copy(3)
             next(ch)
         else:
-            op("v", ["iotf", tok(back)], ["osp"], lambda: V.tensor_copy(by("osp", back), T.iotf[:]))
+            op("s", ["iotf", tok(o_u)], ["osp"], lambda: S.activation(T.osp[:], by("iotf", o_u), COPY))
             load("y", "l_fo", ["osp"], ["fo"], [(T.fo[:, 0:C], T.osp[0:128:16, 0:C])])
             op("v", ["vt"], ["qv"], lambda: V.quantize_mx(T.qv[:, 0:128], T.sv[:, 0:128], T.vt[:, 0:512]))
             new_state(n, back)
-
-    H = C // 2
-    for h in range(2):
-        op("t", ["qv", "xq3"], ["pa%d" % h], lambda: g.tensor.matmul_mx(T.pa[:, 512 * h:512 * h + H], T.qv[:, 0:128], T.sv[:, 0:128], T.xq3[:, H * h:H * h + H], T.xs3[:, H * h:H * h + H], True, True))
-    load("y", "l_oc", ["xq3"], ["oc"], [(T.oc[:, 0:4 * C], T.xq3[:, 0:C].bitcast(dt.uint8))])
-    op("s", ["pa0"], ["ysb0"], lambda: S.activation(T.ysb[:, 0:H], T.pa[:, 0:H], COPY))
-    op("v", ["pa1"], ["ysb1"], lambda: V.tensor_copy(T.ysb[:, H:C], T.pa[:, 512:512 + H]))
-    load("s", "l_y0", ["ysb0"], ["y0"], [(T.y[:, 0:H], T.ysb[:, 0:H])])
-    load("y", "l_y1", ["ysb1"], ["y1"], [(T.y[:, H:C], T.ysb[:, H:C])])
-    load("s", "l_osc", ["xq3"], ["osc"], [(T.osc[4 * k:4 * k + 4, 0:C], T.xs3[32 * k:32 * k + 4, 0:C]) for k in range(4)])
 
     for sem in sorted(totals):
         if seen["g"].get(sem, 0) < totals[sem]:

@@ -3,15 +3,19 @@ from concourse.mybir import dt, AluOpType, ActivationFunctionType
 C = 448
 K = C // 16
 STEP = [1, 2, 3]
-RADIX = [3, 3, 3, 2, 3, 3]
-PRE = 3
-TV1, TV2 = (0, 1, 2), (1, 2, 3, 4)
+RADIX = [3, 3, 2, 3, 3, 3]
+F1 = ((0,), (1,), (2,))
+F2 = (((0, 1),), ((2,), (3,)))
+LATE = 0
+VF0 = False
+PRE = 4
+TV1, TV2 = (0, 1, 2, 3), (1, 2, 4)
 MID = C // 2
 UP = 512.0
 SCN = "float16"
 
 SCRATCH = {
-    "md": ("sbuf", [128, C], "int32"), "rti": ("sbuf", [128, C], "int32"),
+    "md": ("sbuf", [128, C], "int32"), "rti": ("sbuf", [128, C], "bfloat16"), "m4": ("sbuf", [128, 4], "float32"),
     "thr": ("sbuf", [128, C], "float32"), "d0": ("sbuf", [128, C], "bfloat16"),
     "da": ("sbuf", [128, C], "bfloat16"), "db": ("sbuf", [128, C], "bfloat16"),
     "rst": ("sbuf", [128, C], "bfloat16"), "iots": ("sbuf", [128, C], "bfloat16"),
@@ -38,6 +42,7 @@ for _b in range(4):
     SCRATCH["f%d" % _b] = ("sbuf", [128, C], "bfloat16")
     SCRATCH["fd%d" % _b] = ("sbuf", [128, C], "bfloat16")
     SCRATCH["u%d" % _b] = ("sbuf", [128, C], "float32")
+    SCRATCH["gg%d" % _b] = ("sbuf", [128, C], "bfloat16")
     SCRATCH["ld%d" % _b] = ("sbuf", [128, C], "bfloat16")
     SCRATCH["r%d" % _b] = ("sbuf", [128, C], "float32")
     SCRATCH["scn%d" % _b] = ("sbuf", [128, C], SCN)
@@ -57,7 +62,7 @@ for _n in (2, 3):
 
 SEMAPHORES = ["cv", "cs", "ct", "cg", "sent", "a_od"] \
     + ["a_z10", "a_z20", "a_z30", "a_z31"] + ["a_ol%d" % n for n in (2, 3)] \
-    + ["l_" + n for n in ("od", "x", "u", "v", "wc", "ws", "y0", "y1", "fo", "oc0", "oc1", "osc0", "osc1", "f0", "f1", "f2", "f3")]
+    + ["l_" + n for n in ("od", "x", "u", "v", "wc", "ws", "y0", "y1", "fo", "oc0", "oc1", "osc0", "osc1", "f0", "f1", "f2")]
 
 ADD, MUL, SUB, MIN, MAX = AluOpType.add, AluOpType.mult, AluOpType.subtract, AluOpType.min, AluOpType.max
 COPY = ActivationFunctionType.Copy
@@ -125,11 +130,11 @@ def rank_program(g, core, T, topo):
     def bits(engines):
         return sum(1 << e for e in engines)
 
-    def send(step, out, in_, key, sem, few=False):
+    def send(step, out, in_, key, sem, few=None):
         dst = peer(step)
         e = topo.engines(core, dst)
-        if few:
-            e = e[::2]
+        if few is not None:
+            e = e[few::2]
         await_for("g", [key], [])
         rid, pid, _ = topo.addr(dst)
         g.remote_dma(out, in_, T.sem[sem], T.sem["sent"], pid, rid, bits(e))
@@ -176,20 +181,24 @@ def rank_program(g, core, T, topo):
     op("g", [], ["md"], lambda: g.iota(T.md[:], [[1, C]], 128, -1))
     op("g", [], ["iots"], lambda: g.iota(T.iots[:], [[1, C]], -MID, 0, allow_small_or_imprecise_dtypes=True))
     op("v", [], ["ones"], lambda: V.memset(T.ones[:], 1.0))
-    arrives("a_od", send(STEP[0], T.odr[:], T.odl[:], "odl", "a_od", few=True), ["odr"])
+    op("v", [], ["m4a"], lambda: V.memset(T.m4[:, 0:1], -4.0))
+    op("v", [], ["m4b"], lambda: V.memset(T.m4[:, 1:2], 2 * UP))
+    arrives("a_od", send(STEP[0], T.odr[:], T.odl[:], "odl", "a_od", few=0), ["odr"])
     op("g", ["ones"], ["eye"], lambda: g.affine_select(T.eye[:], T.ones[:], [[1, 516]], AluOpType.is_equal, 0.0, -3, -4))
     op("g", [], ["uoi"], lambda: g.iota(T.uoi[:], [[16, 8]], 0, 0))
-    op("g", [], ["rti"], lambda: g.iota(T.rti[:], [[0, K], [1, 16]], 0, 0))
+    op("g", [], ["iotd"], lambda: g.iota(T.iotd[:], [[1, C]], -MID, 0, allow_small_or_imprecise_dtypes=True))
+    op("g", [], ["rti"], lambda: g.iota(T.rti[:], [[0, K], [1, 16]], 0, 0, allow_small_or_imprecise_dtypes=True))
     op("g", [], ["iotf"], lambda: g.iota(T.iotf[:], [[1, C]], 0, 0, allow_small_or_imprecise_dtypes=True))
 
     op("v", ["md"], ["md"], lambda: V.tensor_scalar(T.md[:], T.md[:], 15, None, AluOpType.bitwise_and))
-    op("v", ["md"], ["da"], lambda: V.tensor_scalar(T.da[:], T.md[:], 1.0, UP, AluOpType.is_equal, MUL))
-    op("v", ["md"], ["db"], lambda: V.tensor_scalar(T.db[:], T.md[:], 0.0, -2 * UP, AluOpType.is_equal, MUL))
+    op("v", ["md"], ["da"], lambda: V.tensor_scalar(T.da[:], T.md[:], 2.0, 3.0, MIN, MUL))
+    op("s", ["da", "m4a", "m4b"], ["db"], lambda: S.activation(T.db[:], T.da[:], ActivationFunctionType.Abs, bias=T.m4[:, 0:1]))
+    op("s", ["db"], ["d0"], lambda: S.activation(T.d0[:], T.db[:], ActivationFunctionType.Identity, bias=T.m4[:, 1:2], scale=-UP))
+    op("s", ["da"], ["thr"], lambda: S.activation(T.thr[:], T.da[:], COPY, scale=1e28))
     o_u, o_f = slot(), fslot()
     op("v", ["odl"], [tok(o_u)], lambda: V.tensor_copy(tu(o_u), T.odl[:]))
     op("v", ["odl"], ["tf%d" % o_f], lambda: V.tensor_copy(tf(o_f), T.odl[:]))
     op("v", ["iots", tok(o_u)], ["bk0"], lambda: V.tensor_copy(by("bk0", o_u), T.iots[:]))
-    op("v", ["da", "db"], ["d0"], lambda: V.tensor_tensor(T.d0[:], T.da[:], T.db[:], ADD))
     op("v", ["md"], ["bia0"], lambda: V.tensor_scalar(T.bia[:, 0:1], T.md[:, 15:16], 0.0, UP, AluOpType.is_equal, MUL))
     op("v", ["bia0"], ["bia"], lambda: V.tensor_scalar(T.bia[:, 1:2], T.bia[:, 0:1], MID - UP, None, ADD))
 
@@ -202,7 +211,15 @@ def rank_program(g, core, T, topo):
         op("v", [h, "bia"], [tok(i)], lambda: V.tensor_scalar(tu(i), T[h][:, 15:C:16], T.bia[:, 1:2], None, ADD))
         return i
 
-    out = {}
+    out = {"fill_s": [], "fill_v": []}
+
+    def between(k):
+        if len(out[k]) > 0:
+            out[k].pop(0)()
+
+    def drain(k):
+        while len(out[k]) > 0:
+            out[k].pop(0)()
 
     def chain(n, o_u, o_f, twin_v):
         star = fslot()
@@ -231,9 +248,13 @@ def rank_program(g, core, T, topo):
                 for e in range(r - 1):
                     kn = (kn + 1) % 4
                     new = "kb%d" % kn
+                    between("fill_s")
                     op("s", [cur, tok(a)], [new], lambda: S.activation(T[new][:], by(cur, a), COPY))
                     cur = new
+            drain("fill_s")
             for e in range(r - 1):
+                if e > 0 or VF0:
+                    between("fill_v")
                 ln = (ln + 1) % 4
                 lnew = "lb%d" % ln
                 op("v", [acc, low, tok(a)], [lnew], lambda: V.tensor_tensor(T[lnew][:], by(acc, a), T[low][:], MIN))
@@ -242,11 +263,13 @@ def rank_program(g, core, T, topo):
             kname = cur
             if not last:
                 twin = "ld%d" % (j % 4)
+                between("fill_v")
                 if j in twin_v:
                     a = conv(kname, lambda: op("v", [low], [twin], lambda: V.tensor_copy(T[twin][:], T[low][:])))
                 else:
                     op("s", [low], [twin], lambda: S.activation(T[twin][:], T[low][:], COPY))
                     a = conv(kname)
+            drain("fill_v")
             yield
         out["low"] = conv(low)
         out["delta"] = delta
@@ -257,13 +280,14 @@ def rank_program(g, core, T, topo):
 
     def unpack_products(n):
         xq, xs = "xq%d" % n, "xs%d" % n
-        op("t", ["qur", xq], ["pb0"], lambda: g.tensor.matmul_mx(T.pb[:, 0:C], T.qur[:, 0:128], T.sur[:, 0:128], T[xq][:, 0:C], T[xs][:, 0:C], True, True))
+        op("t", ["qur", "sur", xq], ["pb0"], lambda: g.tensor.matmul_mx(T.pb[:, 0:C], T.qur[:, 0:128], T.sur[:, 0:128], T[xq][:, 0:C], T[xs][:, 0:C], True, True))
         for b in range(4):
             op("t", ["qe%d" % b, xq], ["pa%d" % b], lambda: g.tensor.matmul_mx(T.pa[:, 512 * b:512 * b + C], T.qe[:, 128 * b:128 * b + 128], T.se[:, 128 * b:128 * b + 128], T[xq][:, 0:C], T[xs][:, 0:C], True, True))
 
     def f_copy(b):
         op("s", ["pa%d" % b], ["f%d" % b], lambda: S.activation(T["f%d" % b][:], T.pa[:, 512 * b:512 * b + C], COPY))
-        load("y", "l_f%d" % b, ["f%d" % b], ["fd%d" % b], [(T["fd%d" % b][:], T["f%d" % b][:])])
+        if b < 3:
+            load("y", "l_f%d" % b, ["f%d" % b], ["fd%d" % b], [(T["fd%d" % b][:], T["f%d" % b][:])])
 
     def scores(o_u):
         op("s", ["pb0"], ["sc"], lambda: S.activation(T.sc[:], T.pb[:, 0:C], COPY))
@@ -287,13 +311,19 @@ def rank_program(g, core, T, topo):
 
         if n < len(STEP):
             m = n + 1
-            arrives("a_ol%d" % m, send(STEP[n], T["ol%d" % m][:], tu(o_u), tok(o_u), "a_ol%d" % m, few=True), ["ol%d" % m])
-        for b in range(4):
-            op("v", ["f%d" % b, "fd%d" % b, tok(o_u)], ["u%d" % b], lambda: V.tensor_tensor(T["u%d" % b][:], by("f%d" % b, o_u), T["fd%d" % b][:], ADD))
+            arrives("a_ol%d" % m, send(STEP[n], T["ol%d" % m][:], tu(o_u), tok(o_u), "a_ol%d" % m, few=1), ["ol%d" % m])
+        shared = (3,)
+        for b in shared:
+            op("s", ["f%d" % b, tok(o_u)], ["gg%d" % b], lambda: S.activation(T["gg%d" % b][:], by("f%d" % b, o_u), COPY))
         parts = pieces(n)
         turn = [(b, 0) for b in range(4)]
+        for b in range(4):
+            if b in shared:
+                op("v", ["gg%d" % b, "pa%d" % b], ["u%d" % b], lambda: V.tensor_tensor(T["u%d" % b][:], T["gg%d" % b][:], T.pa[:, 512 * b:512 * b + C], ADD))
+            else:
+                op("v", ["f%d" % b, "fd%d" % b, tok(o_u)], ["u%d" % b], lambda: V.tensor_tensor(T["u%d" % b][:], by("f%d" % b, o_u), T["fd%d" % b][:], ADD))
         if len(parts) == 2:
-            turn = [(0, 0), (1, 0), (0, 1), (2, 0), (1, 1), (3, 0), (2, 1), (3, 1)]
+            turn = [(0, 0), (0, 1), (1, 0), (2, 0), (1, 1), (2, 1)]
         for b, h in turn:
             p, e = parts[h]
             op("s", ["u%d" % b, tok(o_u)], ["zt%d%d" % (b, h)], lambda: S.activation(T.zt[:, 4 * p + b:4 * e:4], T["u%d" % b][:, 0:C].indirect(T.tu[:, K * o_u + p // 16:K * o_u + e // 16]), COPY, scale=0.5))
@@ -302,6 +332,8 @@ def rank_program(g, core, T, topo):
         zq, zs, zl, zp = "zq%d" % n, "zs%d" % n, "zl%d" % n, "zp%d" % n
         for h, (p, e) in enumerate(parts):
             key, sem = "%s%d" % (zq, h), "a_z%d%d" % (n, h)
+            if len(parts) == 2:
+                op("v", ["u3", tok(o_u)], ["zt3%d" % h], lambda: V.tensor_scalar(T.zt[:, 4 * p + 3:4 * e:4], T.u3[:, 0:C].indirect(T.tu[:, K * o_u + p // 16:K * o_u + e // 16]), 0.5, None, MUL))
             op("v", ["zt%d%d" % (b, h) for b in range(4)], [key], lambda: V.quantize_mx(T[zq][:, p:e], T[zs][:, p:e], T.zt[:, 4 * p:4 * e]))
             k = send(STEP[n - 1], T[zl][:, p:e].bitcast(dt.uint8), T[zq][:, p:e].bitcast(dt.uint8), key, sem)
             k += send(STEP[n - 1], T[zp][:, p:e], T[zs][:, p:e], key, sem)
@@ -309,6 +341,22 @@ def rank_program(g, core, T, topo):
         if n == len(STEP):
             inverse()
         return conv(bk)
+
+    def new_state_between(n, back):
+        zl, zp, xq, xs = "zl%d" % n, "zp%d" % n, "xq%d" % n, "xs%d" % n
+
+        def r_copy(b):
+            op("s", ["pb%d" % b], ["r%d0" % b], lambda: S.activation(T["r%d" % b][:], T.pb[:, 512 * b:512 * b + C], COPY, scale=0.03125))
+
+        def x_add(b):
+            op("v", ["r%d0" % b, "f%d" % b, tok(back)], ["xt_%d0" % b], lambda: V.tensor_tensor(T.xt[:, b:4 * C:4], by("r%d" % b, back), T["f%d" % b][:], ADD))
+            if b == 3:
+                op("v", ["xt_%d0" % k for k in range(4)], [xq], lambda: V.quantize_mx(T[xq][:, 0:C], T[xs][:, 0:C], T.xt[:, 0:4 * C]))
+
+        for b in range(4):
+            op("t", ["wq", "wp", "%s0" % zl], ["pb%d" % b], lambda: g.tensor.matmul_mx(T.pb[:, 512 * b:512 * b + C], T.wq[:, 128 * b:128 * b + 128], T.wp[:, 128 * b:128 * b + 128], T[zl][:, 0:C], T[zp][:, 0:C], True, True))
+            out["fill_s"].append(lambda b=b: r_copy(b))
+            out["fill_v"].append(lambda b=b: x_add(b))
 
     def new_state(n, back):
         zl, zp, xq, xs = "zl%d" % n, "zp%d" % n, "xq%d" % n, "xs%d" % n
@@ -334,26 +382,31 @@ def rank_program(g, core, T, topo):
         load("s", "l_osc%d" % h, [key], [], [(T.osc[4 * k:4 * k + 4, p:e], T.xs3[32 * k:32 * k + 4, p:e]) for k in range(4)])
 
     ch = chain(1, o_u, o_f, TV1)
-    next(ch)
-    op("v", ["iots"], ["iotd"], lambda: V.tensor_copy(T.iotd[:], T.iots[:]))
+    if not LATE:
+        next(ch)
     op("v", ["uoi"], ["uo"], lambda: V.tensor_copy(T.uo[:], T.uoi[:]))
     op("v", ["ut"], ["qu"], lambda: V.quantize_mx(T.qu[:, 0:128], T.su[:, 0:128], T.ut[:, 0:512]))
-    op("v", ["qu", "uo"], ["qur_c"], lambda: V.tensor_copy(T.qur[:, 0:128].bitcast(dt.uint32), T.qu[:, 0:128].bitcast(dt.uint32).indirect(T.uo[:, 0:8])))
-    op("v", ["qu", "uo", "qur_c"], ["qur"], lambda: V.tensor_copy(T.sur[:, 0:128], T.su[:, 0:128].indirect(T.uo[:, 0:8])))
-    next(ch)
+    op("v", ["qu", "uo"], ["qur"], lambda: V.tensor_copy(T.qur[:, 0:128].bitcast(dt.uint32), T.qu[:, 0:128].bitcast(dt.uint32).indirect(T.uo[:, 0:8])))
     for b in range(4):
         op("v", ["eye"], ["qe%d" % b], lambda: V.quantize_mx(T.qe[:, 128 * b:128 * b + 128], T.se[:, 128 * b:128 * b + 128], T.eye[:, 3 - b:515 - b]))
+    if LATE:
+        if LATE > 1:
+            op("v", ["xt0"], ["xq0"], lambda: V.quantize_mx(T.xq0[:, 0:C], T.xs0[:, 0:C], T.xt0[:, 0:4 * C]))
+        next(ch)
     next(ch)
-    op("v", ["xt0"], ["xq0"], lambda: V.quantize_mx(T.xq0[:, 0:C], T.xs0[:, 0:C], T.xt0[:, 0:4 * C]))
+    next(ch)
+    op("s", ["rti"], ["rst"], lambda: S.activation(T.rst[:], T.rti[:], ActivationFunctionType.Sign))
+    op("s", ["qu", "uo"], ["sur"], lambda: S.activation(T.sur[:, 0:128], T.su[:, 0:128].indirect(T.uo[:, 0:8]), COPY))
+    if LATE < 2:
+        op("v", ["xt0"], ["xq0"], lambda: V.quantize_mx(T.xq0[:, 0:C], T.xs0[:, 0:C], T.xt0[:, 0:4 * C]))
     unpack_products(0)
-    for b in range(4):
-        if b > 0:
-            next(ch)
-        f_copy(b)
-    op("v", ["md"], ["thr"], lambda: V.tensor_scalar(T.thr[:], T.md[:], 1.0, 1e29, MIN, MUL))
-    op("v", ["rti"], ["rst"], lambda: V.tensor_scalar(T.rst[:], T.rti[:], 1.0, None, MIN))
+    for fs in F1:
+        next(ch)
+        for b in fs:
+            f_copy(b)
     next(ch)
     scores(o_u)
+    f_copy(3)
     next(ch)
     next(ch)
 
@@ -364,18 +417,18 @@ def rank_program(g, core, T, topo):
             ch = chain(n + 1, o_u, o_f, TV2)
             for _ in range(PRE):
                 next(ch)
-            new_state(n, back)
+            new_state_between(n, back)
+            next(ch)
             unpack_products(n)
-            for b in range(2):
-                if 3 + b >= PRE:
-                    next(ch)
-                f_copy(b)
-            next(ch)
+            for fs in F2[0]:
+                next(ch)
+                for b in fs:
+                    f_copy(b)
             scores(o_u)
-            f_copy(2)
-            next(ch)
-            f_copy(3)
-            next(ch)
+            for fs in F2[1]:
+                for b in fs:
+                    f_copy(b)
+                next(ch)
         else:
             op("s", ["iotf", tok(o_u)], ["osp"], lambda: S.activation(T.osp[:], by("iotf", o_u), COPY))
             load("y", "l_fo", ["osp"], ["fo"], [(T.fo[:, 0:C], T.osp[0:128:16, 0:C])])

from concourse.mybir import dt, AluOpType, ActivationFunctionType

C = 448
K = C // 16
STEP = [1, 2, 3]
RADIX = [3, 3, 2, 3, 3, 3]
F1 = ((0,), (1,), (2,))
F2 = (((0, 1),), ((2,), (3,)))
LATE = 0
VF0 = False
PRE = 4
TV1, TV2 = (0, 1, 2, 3), (1, 2, 4)
MID = C // 2
UP = 512.0
SCN = "float16"

SCRATCH = {
    "md": ("sbuf", [128, C], "int32"), "rti": ("sbuf", [128, C], "bfloat16"), "m4": ("sbuf", [128, 4], "float32"),
    "thr": ("sbuf", [128, C], "float32"), "d0": ("sbuf", [128, C], "bfloat16"),
    "da": ("sbuf", [128, C], "bfloat16"), "db": ("sbuf", [128, C], "bfloat16"),
    "rst": ("sbuf", [128, C], "bfloat16"), "iots": ("sbuf", [128, C], "bfloat16"),
    "iotd": ("sbuf", [128, C], "bfloat16"), "iotf": ("sbuf", [128, C], "float32"), "ones": ("sbuf", [128, 516], "bfloat16"),
    "eye": ("sbuf", [128, 516], "bfloat16"), "bia": ("sbuf", [128, 4], "float32"),
    "uoi": ("sbuf", [128, 8], "int32"), "uo": ("sbuf", [128, 8], "uint16"),
    "odl": ("sbuf", [128, K], "int32"), "ut": ("sbuf", [128, 512], "bfloat16"),
    "vt": ("sbuf", [128, 512], "bfloat16"), "xt0": ("sbuf", [128, 4 * C], "bfloat16"),
    "qu": ("sbuf", [128, 128], "float8_e4m3fn_x4"), "su": ("sbuf", [128, 128], "uint8"),
    "qur": ("sbuf", [128, 128], "float8_e4m3fn_x4"), "sur": ("sbuf", [128, 128], "uint8"),
    "qv": ("sbuf", [128, 128], "float8_e4m3fn_x4"), "sv": ("sbuf", [128, 128], "uint8"),
    "qe": ("sbuf", [128, 512], "float8_e4m3fn_x4"), "se": ("sbuf", [128, 512], "uint8"),
    "wq": ("sbuf", [128, 512], "float8_e4m3fn_x4"), "wp": ("sbuf", [128, 512], "uint8"),
    "odr": ("sbuf", [128, K], "int32"),
    "sc": ("sbuf", [128, C], "float32"), "so": ("sbuf", [128, C], "float32"),
    "dm": ("sbuf", [128, C], "bfloat16"), "ds": ("sbuf", [128, C], "bfloat16"),

    "zt": ("sbuf", [128, 4 * C], "bfloat16"), "xt": ("sbuf", [128, 4 * C], "bfloat16"),
    "ysb": ("sbuf", [128, C], "float32"), "osp": ("sbuf", [128, C], "float32"),
    "tu": ("sbuf", [128, K * 40], "uint16"), "tf": ("sbuf", [128, K * 20], "float32"),
    "pa": ("psum", [128, 2048], "float32"), "pb": ("psum", [128, 2048], "float32"),
}
for _b in range(4):
    SCRATCH["f%d" % _b] = ("sbuf", [128, C], "bfloat16")
    SCRATCH["fd%d" % _b] = ("sbuf", [128, C], "bfloat16")
    SCRATCH["u%d" % _b] = ("sbuf", [128, C], "float32")
    SCRATCH["gg%d" % _b] = ("sbuf", [128, C], "bfloat16")
    SCRATCH["ld%d" % _b] = ("sbuf", [128, C], "bfloat16")
    SCRATCH["r%d" % _b] = ("sbuf", [128, C], "float32")
    SCRATCH["scn%d" % _b] = ("sbuf", [128, C], SCN)
    SCRATCH["kb%d" % _b] = ("sbuf", [128, C], "bfloat16")
    SCRATCH["lb%d" % _b] = ("sbuf", [128, C], "bfloat16")
    SCRATCH["xq%d" % _b] = ("sbuf", [128, C], "float8_e4m3fn_x4")
    SCRATCH["xs%d" % _b] = ("sbuf", [128, C], "uint8")
SCRATCH["bk0"] = ("sbuf", [128, C], "bfloat16")
for _n in (1, 2, 3):
    SCRATCH["zq%d" % _n] = ("sbuf", [128, C], "float8_e4m3fn_x4")
    SCRATCH["zs%d" % _n] = ("sbuf", [128, C], "uint8")
    SCRATCH["zl%d" % _n] = ("sbuf", [128, C], "float8_e4m3fn_x4")
    SCRATCH["zp%d" % _n] = ("sbuf", [128, C], "uint8")
    SCRATCH["bk%d" % _n] = ("sbuf", [128, C], "bfloat16")
for _n in (2, 3):
    SCRATCH["ol%d" % _n] = ("sbuf", [128, K], "uint16")

SEMAPHORES = ["cv", "cs", "ct", "cg", "sent", "a_od"] \
    + ["a_z10", "a_z20", "a_z30", "a_z31"] + ["a_ol%d" % n for n in (2, 3)] \
    + ["l_" + n for n in ("od", "x", "u", "v", "wc", "ws", "y0", "y1", "fo", "oc0", "oc1", "osc0", "osc1", "f0", "f1", "f2")]

ADD, MUL, SUB, MIN, MAX = AluOpType.add, AluOpType.mult, AluOpType.subtract, AluOpType.min, AluOpType.max
COPY = ActivationFunctionType.Copy


def rank_program(g, core, T, topo):
    rank = T.rank_of(core)
    if rank is None:
        return
    queues = {"v": g.vector, "s": g.scalar, "t": g.tensor, "g": g, "y": g.sync}
    count = {"v": 0, "s": 0, "t": 0, "g": 0}
    wrote, read, snap = {}, {}, {}
    seen = {q: {} for q in queues}
    totals = {}

    def learn(q, sem, val):
        s = seen[q]
        if s.get(sem, 0) < val:
            s[sem] = val
        for a, b in snap.get((sem, val), {}).items():
            if s.get(a, 0) < b:
                s[a] = b

    def await_for(q, reads, writes):
        need = {}
        for k in reads:
            for sem, val in wrote.get(k, []):
                need[sem] = max(need.get(sem, 0), val)
        for k in writes:
            for sem, val in wrote.get(k, []):
                need[sem] = max(need.get(sem, 0), val)
            for sem, val in read.get(k, []):
                need[sem] = max(need.get(sem, 0), val)
        for sem in sorted(need):
            if seen[q].get(sem, 0) < need[sem]:
                queues[q].wait_ge(T.sem[sem], need[sem])
                learn(q, sem, need[sem])

    def note(q, tok, reads, writes):
        snap[tok] = dict(seen[q])
        for k in reads:
            read.setdefault(k, []).append(tok)
        for k in writes:
            wrote[k] = [tok]
            read[k] = []

    def op(q, reads, writes, call):
        await_for(q, reads, writes)
        count[q] += 1
        sem = "c" + q
        call().then_inc(T.sem[sem], 1)
        totals[sem] = count[q]
        note(q, (sem, count[q]), reads, writes)

    def load(q, sem, reads, writes, pairs):
        await_for(q, reads, writes)
        for out, in_ in pairs:
            queues[q].dma_start(out, in_).then_inc(T.sem[sem], 16)
            totals[sem] = totals.get(sem, 0) + 16
        note(q, (sem, totals[sem]), reads, writes)

    def peer(step):
        return T.cores[rank ^ step]

    def bits(engines):
        return sum(1 << e for e in engines)

    def send(step, out, in_, key, sem, few=None):
        dst = peer(step)
        e = topo.engines(core, dst)
        if few is not None:
            e = e[few::2]
        await_for("g", [key], [])
        rid, pid, _ = topo.addr(dst)
        g.remote_dma(out, in_, T.sem[sem], T.sem["sent"], pid, rid, bits(e))
        totals["sent"] = totals.get("sent", 0) + len(e)
        return len(e)

    def arrives(sem, engines, keys):
        totals[sem] = totals.get(sem, 0) + engines
        for k in keys:
            wrote[k] = [(sem, totals[sem])]
        if len(keys) > 0:
            snap.setdefault((sem, totals[sem]), {})

    V, S = g.vector, g.scalar
    slots, fslots = [0], [0]

    def slot():
        slots[0] += 1
        return slots[0] - 1

    def fslot():
        fslots[0] += 1
        return fslots[0] - 1

    def tu(i):
        return T.tu[:, K * i:K * (i + 1)]

    def tf(i):
        return T.tf[:, K * i:K * (i + 1)]

    def by(name, i):
        return T[name][:, 0:C].indirect(tu(i))

    def tok(i):
        return "tu%d" % i

    load("y", "l_od", [], ["odl"], [(T.odl[:], T.od[:])])
    load("y", "l_u", [], ["ut"], [(T.ut[:], T.u[:])])
    load("y", "l_x", [], ["xt0"], [(T.xt0[:], T.x[:])])
    load("y", "l_wc", [], ["wq"], [(T.wq[:, 0:512].bitcast(dt.uint8), T.wc[:, 0:2048])])
    load("y", "l_ws", [], ["wp"], [(T.wp[:, 0:512], T.ws[:, 0:512])])
    load("y", "l_v", [], ["vt"], [(T.vt[:], T.v[:])])

    op("g", [], ["md"], lambda: g.iota(T.md[:], [[1, C]], 128, -1))
    op("g", [], ["iots"], lambda: g.iota(T.iots[:], [[1, C]], -MID, 0, allow_small_or_imprecise_dtypes=True))
    op("v", [], ["ones"], lambda: V.memset(T.ones[:], 1.0))
    op("v", [], ["m4a"], lambda: V.memset(T.m4[:, 0:1], -4.0))
    op("v", [], ["m4b"], lambda: V.memset(T.m4[:, 1:2], 2 * UP))
    arrives("a_od", send(STEP[0], T.odr[:], T.odl[:], "odl", "a_od", few=0), ["odr"])
    op("g", ["ones"], ["eye"], lambda: g.affine_select(T.eye[:], T.ones[:], [[1, 516]], AluOpType.is_equal, 0.0, -3, -4))
    op("g", [], ["uoi"], lambda: g.iota(T.uoi[:], [[16, 8]], 0, 0))
    op("g", [], ["iotd"], lambda: g.iota(T.iotd[:], [[1, C]], -MID, 0, allow_small_or_imprecise_dtypes=True))
    op("g", [], ["rti"], lambda: g.iota(T.rti[:], [[0, K], [1, 16]], 0, 0, allow_small_or_imprecise_dtypes=True))
    op("g", [], ["iotf"], lambda: g.iota(T.iotf[:], [[1, C]], 0, 0, allow_small_or_imprecise_dtypes=True))

    op("v", ["md"], ["md"], lambda: V.tensor_scalar(T.md[:], T.md[:], 15, None, AluOpType.bitwise_and))
    op("v", ["md"], ["da"], lambda: V.tensor_scalar(T.da[:], T.md[:], 2.0, 3.0, MIN, MUL))
    op("s", ["da", "m4a", "m4b"], ["db"], lambda: S.activation(T.db[:], T.da[:], ActivationFunctionType.Abs, bias=T.m4[:, 0:1]))
    op("s", ["db"], ["d0"], lambda: S.activation(T.d0[:], T.db[:], ActivationFunctionType.Identity, bias=T.m4[:, 1:2], scale=-UP))
    op("s", ["da"], ["thr"], lambda: S.activation(T.thr[:], T.da[:], COPY, scale=1e28))
    o_u, o_f = slot(), fslot()
    op("v", ["odl"], [tok(o_u)], lambda: V.tensor_copy(tu(o_u), T.odl[:]))
    op("v", ["odl"], ["tf%d" % o_f], lambda: V.tensor_copy(tf(o_f), T.odl[:]))
    op("v", ["iots", tok(o_u)], ["bk0"], lambda: V.tensor_copy(by("bk0", o_u), T.iots[:]))
    op("v", ["md"], ["bia0"], lambda: V.tensor_scalar(T.bia[:, 0:1], T.md[:, 15:16], 0.0, UP, AluOpType.is_equal, MUL))
    op("v", ["bia0"], ["bia"], lambda: V.tensor_scalar(T.bia[:, 1:2], T.bia[:, 0:1], MID - UP, None, ADD))

    def conv(name, between=None):
        i = slot()
        h = "scn%d" % (i % 4)
        op("v", [name, "d0"], [h], lambda: V.tensor_tensor_scan(T[h][:], T.d0[:], T[name][:], 0.0, ADD, MAX))
        if between is not None:
            between()
        op("v", [h, "bia"], [tok(i)], lambda: V.tensor_scalar(tu(i), T[h][:, 15:C:16], T.bia[:, 1:2], None, ADD))
        return i

    out = {"fill_s": [], "fill_v": []}

    def between(k):
        if len(out[k]) > 0:
            out[k].pop(0)()

    def drain(k):
        while len(out[k]) > 0:
            out[k].pop(0)()

    def chain(n, o_u, o_f, twin_v):
        star = fslot()
        delta = fslot()
        bk = "bk%d" % (n - 1)
        src = "odr" if n == 1 else "ol%d" % n
        offs, okey = T[src][:, 0:K], src
        if n == 1:
            su = slot()
            op("v", ["odr"], [tok(su)], lambda: V.tensor_copy(tu(su), T.odr[:]))
            offs, okey = tu(su), tok(su)
        kn, kname = 0, "kb0"
        op("s", [bk, okey], [kname], lambda: S.activation(T[kname][:], T[bk][:, 0:C].indirect(offs), COPY))
        if n == 1:
            yield
        a = conv(kname)
        op("v", [src], ["tf%d" % star], lambda: V.tensor_copy(tf(star), T[src][:]))
        op("v", ["tf%d" % star, "tf%d" % o_f], ["tf%d" % delta], lambda: V.tensor_tensor(tf(delta), tf(star), tf(o_f), SUB))
        yield
        low, ln, twin = "iots", 0, "iotd"
        for j, r in enumerate(RADIX):
            last = j == len(RADIX) - 1
            acc = twin
            cur = kname
            if not last:
                for e in range(r - 1):
                    kn = (kn + 1) % 4
                    new = "kb%d" % kn
                    between("fill_s")
                    op("s", [cur, tok(a)], [new], lambda: S.activation(T[new][:], by(cur, a), COPY))
                    cur = new
            drain("fill_s")
            for e in range(r - 1):
                if e > 0 or VF0:
                    between("fill_v")
                ln = (ln + 1) % 4
                lnew = "lb%d" % ln
                op("v", [acc, low, tok(a)], [lnew], lambda: V.tensor_tensor(T[lnew][:], by(acc, a), T[low][:], MIN))
                acc = lnew
            low = acc
            kname = cur
            if not last:
                twin = "ld%d" % (j % 4)
                between("fill_v")
                if j in twin_v:
                    a = conv(kname, lambda: op("v", [low], [twin], lambda: V.tensor_copy(T[twin][:], T[low][:])))
                else:
                    op("s", [low], [twin], lambda: S.activation(T[twin][:], T[low][:], COPY))
                    a = conv(kname)
            drain("fill_v")
            yield
        out["low"] = conv(low)
        out["delta"] = delta
        yield

    def pieces(n):
        return [(0, C)] if n < len(STEP) else [(0, C // 2), (C // 2, C)]

    def unpack_products(n):
        xq, xs = "xq%d" % n, "xs%d" % n
        op("t", ["qur", "sur", xq], ["pb0"], lambda: g.tensor.matmul_mx(T.pb[:, 0:C], T.qur[:, 0:128], T.sur[:, 0:128], T[xq][:, 0:C], T[xs][:, 0:C], True, True))
        for b in range(4):
            op("t", ["qe%d" % b, xq], ["pa%d" % b], lambda: g.tensor.matmul_mx(T.pa[:, 512 * b:512 * b + C], T.qe[:, 128 * b:128 * b + 128], T.se[:, 128 * b:128 * b + 128], T[xq][:, 0:C], T[xs][:, 0:C], True, True))

    def f_copy(b):
        op("s", ["pa%d" % b], ["f%d" % b], lambda: S.activation(T["f%d" % b][:], T.pa[:, 512 * b:512 * b + C], COPY))
        if b < 3:
            load("y", "l_f%d" % b, ["f%d" % b], ["fd%d" % b], [(T["fd%d" % b][:], T["f%d" % b][:])])

    def scores(o_u):
        op("s", ["pb0"], ["sc"], lambda: S.activation(T.sc[:], T.pb[:, 0:C], COPY))
        op("s", ["sc", tok(o_u)], ["so"], lambda: S.activation(T.so[:], by("sc", o_u), COPY))

    def choose(o_f):
        low, delta = out["low"], out["delta"]
        t, nf, nu = fslot(), fslot(), slot()
        op("v", ["so", "thr", tok(low)], ["dm"], lambda: V.tensor_tensor(T.dm[:], by("so", low), T.thr[:], AluOpType.is_gt))
        op("v", ["dm", "rst"], ["ds"], lambda: V.tensor_tensor_scan(T.ds[:], T.rst[:], T.dm[:], 0.0, MUL, ADD))
        op("v", ["ds", "tf%d" % delta], ["tf%d" % t], lambda: V.tensor_tensor(tf(t), T.ds[:, 15:C:16], tf(delta), MUL))
        op("v", ["tf%d" % t, "tf%d" % o_f], ["tf%d" % nf], lambda: V.tensor_tensor(tf(nf), tf(t), tf(o_f), ADD))
        op("v", ["tf%d" % nf], [tok(nu)], lambda: V.tensor_copy(tu(nu), tf(nf)))
        return nu, nf

    def means(n, o_u):
        bk = "bk%d" % n

        def inverse():
            op("v", ["iots", tok(o_u)], [bk], lambda: V.tensor_copy(by(bk, o_u), T.iots[:]))

        if n < len(STEP):
            m = n + 1
            arrives("a_ol%d" % m, send(STEP[n], T["ol%d" % m][:], tu(o_u), tok(o_u), "a_ol%d" % m, few=1), ["ol%d" % m])
        shared = (3,)
        for b in shared:
            op("s", ["f%d" % b, tok(o_u)], ["gg%d" % b], lambda: S.activation(T["gg%d" % b][:], by("f%d" % b, o_u), COPY))
        parts = pieces(n)
        turn = [(b, 0) for b in range(4)]
        for b in range(4):
            if b in shared:
                op("v", ["gg%d" % b, "pa%d" % b], ["u%d" % b], lambda: V.tensor_tensor(T["u%d" % b][:], T["gg%d" % b][:], T.pa[:, 512 * b:512 * b + C], ADD))
            else:
                op("v", ["f%d" % b, "fd%d" % b, tok(o_u)], ["u%d" % b], lambda: V.tensor_tensor(T["u%d" % b][:], by("f%d" % b, o_u), T["fd%d" % b][:], ADD))
        if len(parts) == 2:
            turn = [(0, 0), (0, 1), (1, 0), (2, 0), (1, 1), (2, 1)]
        for b, h in turn:
            p, e = parts[h]
            op("s", ["u%d" % b, tok(o_u)], ["zt%d%d" % (b, h)], lambda: S.activation(T.zt[:, 4 * p + b:4 * e:4], T["u%d" % b][:, 0:C].indirect(T.tu[:, K * o_u + p // 16:K * o_u + e // 16]), COPY, scale=0.5))
        if n < len(STEP):
            inverse()
        zq, zs, zl, zp = "zq%d" % n, "zs%d" % n, "zl%d" % n, "zp%d" % n
        for h, (p, e) in enumerate(parts):
            key, sem = "%s%d" % (zq, h), "a_z%d%d" % (n, h)
            if len(parts) == 2:
                op("v", ["u3", tok(o_u)], ["zt3%d" % h], lambda: V.tensor_scalar(T.zt[:, 4 * p + 3:4 * e:4], T.u3[:, 0:C].indirect(T.tu[:, K * o_u + p // 16:K * o_u + e // 16]), 0.5, None, MUL))
            op("v", ["zt%d%d" % (b, h) for b in range(4)], [key], lambda: V.quantize_mx(T[zq][:, p:e], T[zs][:, p:e], T.zt[:, 4 * p:4 * e]))
            k = send(STEP[n - 1], T[zl][:, p:e].bitcast(dt.uint8), T[zq][:, p:e].bitcast(dt.uint8), key, sem)
            k += send(STEP[n - 1], T[zp][:, p:e], T[zs][:, p:e], key, sem)
            arrives(sem, k, ["%s%d" % (zl, h)])
        if n == len(STEP):
            inverse()
        return conv(bk)

    def new_state_between(n, back):
        zl, zp, xq, xs = "zl%d" % n, "zp%d" % n, "xq%d" % n, "xs%d" % n

        def r_copy(b):
            op("s", ["pb%d" % b], ["r%d0" % b], lambda: S.activation(T["r%d" % b][:], T.pb[:, 512 * b:512 * b + C], COPY, scale=0.03125))

        def x_add(b):
            op("v", ["r%d0" % b, "f%d" % b, tok(back)], ["xt_%d0" % b], lambda: V.tensor_tensor(T.xt[:, b:4 * C:4], by("r%d" % b, back), T["f%d" % b][:], ADD))
            if b == 3:
                op("v", ["xt_%d0" % k for k in range(4)], [xq], lambda: V.quantize_mx(T[xq][:, 0:C], T[xs][:, 0:C], T.xt[:, 0:4 * C]))

        for b in range(4):
            op("t", ["wq", "wp", "%s0" % zl], ["pb%d" % b], lambda: g.tensor.matmul_mx(T.pb[:, 512 * b:512 * b + C], T.wq[:, 128 * b:128 * b + 128], T.wp[:, 128 * b:128 * b + 128], T[zl][:, 0:C], T[zp][:, 0:C], True, True))
            out["fill_s"].append(lambda b=b: r_copy(b))
            out["fill_v"].append(lambda b=b: x_add(b))

    def new_state(n, back):
        zl, zp, xq, xs = "zl%d" % n, "zp%d" % n, "xq%d" % n, "xs%d" % n
        parts = pieces(n)
        for h, (p, e) in enumerate(parts):
            bank = "pb" if h == 0 else "pa"
            for b in range(4):
                op("t", ["wq", "wp", "%s%d" % (zl, h)], ["%s%d" % (bank, b)], lambda: g.tensor.matmul_mx(T[bank][:, 512 * b:512 * b + e - p], T.wq[:, 128 * b:128 * b + 128], T.wp[:, 128 * b:128 * b + 128], T[zl][:, p:e], T[zp][:, p:e], True, True))
                op("s", ["%s%d" % (bank, b)], ["r%d%d" % (b, h)], lambda: S.activation(T["r%d" % b][:, p:e], T[bank][:, 512 * b:512 * b + e - p], COPY, scale=0.03125))
        for h, (p, e) in enumerate(parts):
            for b in range(4):
                op("v", ["r%d%d" % (b, k) for k in range(2)] + ["f%d" % b, tok(back)], ["xt_%d%d" % (b, h)], lambda: V.tensor_tensor(T.xt[:, 4 * p + b:4 * e:4], T["r%d" % b][:, 0:C].indirect(T.tu[:, K * back + p // 16:K * back + e // 16]), T["f%d" % b][:, p:e], ADD))
            op("v", ["xt_%d%d" % (b, h) for b in range(4)], [xq if n < len(STEP) else "%s%d" % (xq, h)], lambda: V.quantize_mx(T[xq][:, p:e], T[xs][:, p:e], T.xt[:, 4 * p:4 * e]))
            if n == len(STEP):
                results(h, p, e)

    def results(h, p, e):
        key, bank = "xq3%d" % h, "pb%d" % h
        op("t", ["qv", key], [bank], lambda: g.tensor.matmul_mx(T.pb[:, 512 * h:512 * h + e - p], T.qv[:, 0:128], T.sv[:, 0:128], T.xq3[:, p:e], T.xs3[:, p:e], True, True))
        load("y", "l_oc%d" % h, [key], [], [(T.oc[:, 4 * p:4 * e], T.xq3[:, p:e].bitcast(dt.uint8))])
        op("s", [bank], ["ysb%d" % h], lambda: S.activation(T.ysb[:, p:e], T.pb[:, 512 * h:512 * h + e - p], COPY))
        load("y", "l_y%d" % h, ["ysb%d" % h], [], [(T.y[:, p:e], T.ysb[:, p:e])])
        load("s", "l_osc%d" % h, [key], [], [(T.osc[4 * k:4 * k + 4, p:e], T.xs3[32 * k:32 * k + 4, p:e]) for k in range(4)])

    ch = chain(1, o_u, o_f, TV1)
    if not LATE:
        next(ch)
    op("v", ["uoi"], ["uo"], lambda: V.tensor_copy(T.uo[:], T.uoi[:]))
    op("v", ["ut"], ["qu"], lambda: V.quantize_mx(T.qu[:, 0:128], T.su[:, 0:128], T.ut[:, 0:512]))
    op("v", ["qu", "uo"], ["qur"], lambda: V.tensor_copy(T.qur[:, 0:128].bitcast(dt.uint32), T.qu[:, 0:128].bitcast(dt.uint32).indirect(T.uo[:, 0:8])))
    for b in range(4):
        op("v", ["eye"], ["qe%d" % b], lambda: V.quantize_mx(T.qe[:, 128 * b:128 * b + 128], T.se[:, 128 * b:128 * b + 128], T.eye[:, 3 - b:515 - b]))
    if LATE:
        if LATE > 1:
            op("v", ["xt0"], ["xq0"], lambda: V.quantize_mx(T.xq0[:, 0:C], T.xs0[:, 0:C], T.xt0[:, 0:4 * C]))
        next(ch)
    next(ch)
    next(ch)
    op("s", ["rti"], ["rst"], lambda: S.activation(T.rst[:], T.rti[:], ActivationFunctionType.Sign))
    op("s", ["qu", "uo"], ["sur"], lambda: S.activation(T.sur[:, 0:128], T.su[:, 0:128].indirect(T.uo[:, 0:8]), COPY))
    if LATE < 2:
        op("v", ["xt0"], ["xq0"], lambda: V.quantize_mx(T.xq0[:, 0:C], T.xs0[:, 0:C], T.xt0[:, 0:4 * C]))
    unpack_products(0)
    for fs in F1:
        next(ch)
        for b in fs:
            f_copy(b)
    next(ch)
    scores(o_u)
    f_copy(3)
    next(ch)
    next(ch)

    for n in (1, 2, 3):
        o_u, o_f = choose(o_f)
        back = means(n, o_u)
        if n < 3:
            ch = chain(n + 1, o_u, o_f, TV2)
            for _ in range(PRE):
                next(ch)
            new_state_between(n, back)
            next(ch)
            unpack_products(n)
            for fs in F2[0]:
                next(ch)
                for b in fs:
                    f_copy(b)
            scores(o_u)
            for fs in F2[1]:
                for b in fs:
                    f_copy(b)
                next(ch)
        else:
            op("s", ["iotf", tok(o_u)], ["osp"], lambda: S.activation(T.osp[:], by("iotf", o_u), COPY))
            load("y", "l_fo", ["osp"], ["fo"], [(T.fo[:, 0:C], T.osp[0:128:16, 0:C])])
            op("v", ["vt"], ["qv"], lambda: V.quantize_mx(T.qv[:, 0:128], T.sv[:, 0:128], T.vt[:, 0:512]))
            new_state(n, back)

    for sem in sorted(totals):
        if seen["g"].get(sem, 0) < totals[sem]:
            g.wait_ge(T.sem[sem], totals[sem])
